import numpy as np, ml_dtypes
CORES = [78,86,94,102,110,118]
N = 6
import mx_ref
BF = ml_dtypes.bfloat16
def cols(t, e):
    v = np.concatenate([t.reshape(128, -1, 4), np.zeros((128, 1, 4), BF)], axis=1)
    return np.ascontiguousarray(v[:, e]).reshape(128, -1)
def decode(q):
    o = []
    for b in range(4):
        e = np.zeros((128, 128, 4), np.float32); e[np.arange(128), np.arange(128), b] = 1
        o.append(mx_ref.matmul(mx_ref.quantize(e.reshape(128, 512).astype(BF)), q))
    return np.stack(o, axis=2).reshape(128, -1)
def f(rng, *shape):
    return mx_ref.flush((rng.standard_normal(shape, dtype=np.float32) * np.exp2(rng.integers(-2, 3, shape[:-1] + (1,)))).astype(BF))
def wide(rng, *shape, cols=0):
    v = rng.standard_normal(shape, dtype=np.float32) * np.exp2(rng.integers(-12, 13, shape)).astype(np.float32)
    if cols: v *= np.repeat(np.exp2(rng.integers(-cols, cols + 1, shape[:-2] + (1, shape[-1] // 4))) * (rng.random(shape[:-2] + (1, shape[-1] // 4)) > 0.0625), 4, axis=-1).astype(np.float32)
    return mx_ref.flush(v.astype(BF))
T, K = 512, 160
def setup_inputs(rng):
    u = np.zeros((N, 128, 512), BF); u[:, :, :4] = f(rng, N, 128, 4)
    return {"gr": f(rng, N, 128, 4 * T), "u": u}
def raised(rng, chosen):
    d = setup_inputs(rng)
    for r in range(N):
        g = d["gr"][r].astype(np.float32).reshape(128, T, 4)
        sign = np.where(d["u"][r][:, :4].astype(np.float32) < 0, -1, 1).reshape(128, 1, 4) * rng.choice([-1, 1], K).reshape(1, K, 1)
        v = g * np.float32(2.0 ** -8)
        v[:, chosen[r]] = np.abs(g[:, chosen[r]]) * sign
        d["gr"][r] = mx_ref.flush(v.reshape(128, 4 * T).astype(BF))
    return d
def setup_inputs_same(rng):
    d = raised(rng, [rng.permutation(T)[:K]] * N)
    k = rng.permutation(np.concatenate([[12, -12, -11], rng.integers(-12, 13, N - 3)]))
    d["gr"] = mx_ref.flush((d["gr"].astype(np.float32) * np.exp2(k).astype(np.float32).reshape(N, 1, 1)).astype(BF))
    return d
def setup_inputs_apart(rng):
    p = rng.permutation(T)
    return raised(rng, [p[(r * K + np.arange(K)) % T] for r in range(N)])
def setup_inputs_ties(rng):
    d = setup_inputs(rng); n = T // 11
    for r in range(N):
        p = rng.permutation(T)[:11 * n]
        e = np.full(T, -1); e[p] = np.repeat(np.arange(n), 11)
        s = rng.choice([-1, 1], (n, 11)); s[:, 0] = 1; s[:, 1] = -1
        sign = np.ones(T, np.float32); sign[p] = s.reshape(-1)
        d["gr"][r] = (cols(d["gr"][r], e).astype(np.float32).reshape(128, T, 4) * sign.reshape(1, T, 1)).reshape(128, 4 * T).astype(BF)
    return d
def setup_inputs_few(rng):
    d = setup_inputs(rng); p = rng.permutation(N)
    d["u"][p[0]] = 0
    sign = rng.choice([-1, 1], (128, 1, 4))
    d["u"][p[1]][:, :4] = (sign * rng.uniform(1, 4, (128, 1, 4)) * 2.0 ** 28).reshape(128, 4).astype(BF)
    d["gr"][p[1]] = (sign * rng.choice([-1, 1], (1, T, 1)) * rng.uniform(1, 4, (128, T, 4)) * 2.0 ** 28).reshape(128, 4 * T).astype(BF)
    for r in p[2:2 + N // 2]:
        k = rng.permutation(T)[:rng.integers(1, K)]
        e = np.full(T, -1); e[k] = k
        d["gr"][r] = cols(d["gr"][r], e)
    return d
def setup_inputs_spread(rng):
    d = setup_inputs(rng); d["gr"] = wide(rng, N, 128, 4 * T, cols=8); return d
def check_inputs(d):
    return ["u"] if (d["u"][:, :, 4:].astype(np.float32) != 0).any() else []
def reference(gr, u):
    acc = np.zeros((128, T, 4), np.float32); nb = np.zeros((N, K), np.float32); sc = np.zeros((N, 1, K), np.float32)
    er = gr.astype(np.float32).reshape(N, 128, T, 4)
    for s in range(N):
        score = np.abs(mx_ref.matmul(mx_ref.quantize(u[s]), mx_ref.quantize(gr[s]))[0]) + np.float32(0.0)
        e = np.argsort(-score, kind="stable")[:K]
        v = decode(mx_ref.quantize(cols(gr[s], e))).reshape(128, K, 4)
        acc[:, e] = acc[:, e] + v
        er[s][:, e] = er[s][:, e] - v
        nb[s] = e
        sc[s, 0] = score[e]
    return {"acc": np.stack([acc.reshape(128, 4 * T)] * N), "er": er.reshape(N, 128, 4 * T), "nb": np.stack([nb] * N), "sc": sc}

@@ -1,0 +1,492 @@
+from concourse.bass import DstId, RemoteDMATransfer
+from concourse.mybir import dt, AluOpType, ActivationFunctionType
+
+N, TC, K = 6, 512, 160
+W = 8 + N * K
+L = K // 16
+SHARE = [(3, 1, 1)] + [(2, 2, 1)] * (N - 1)
+
+F, B, I, U, C8, P8 = "float32", "bfloat16", "int32", "uint16", "float8_e4m3fn_x4", "uint8"
+SCRATCH = {
+    "U4": ("sbuf", [128, 16], B), "UT": ("sbuf", [128, 512], B),
+    "UQ": ("sbuf", [128, 128], C8), "UP": ("sbuf", [128, 128], P8),
+    "GR": ("sbuf", [128, 2048], B), "GQ": ("sbuf", [128, 512], C8), "GP": ("sbuf", [128, 512], P8),
+    "ON": ("sbuf", [128, 640], B), "MM": ("sbuf", [128, 516], B),
+    "EQ": ("sbuf", [128, 512], C8), "EP": ("sbuf", [128, 512], P8),
+    "PS": ("psum", [128, 4096], F),
+    "SR": ("sbuf", [128, 512], F), "SL": ("sbuf", [128, 512], F), "SCO": ("sbuf", [128, 4], F), "SN": ("sbuf", [128, 4], F),
+    "SG": ("sbuf", [128, 1024], B), "CM": ("sbuf", [128, 2560], B), "CN": ("sbuf", [128, 1280], B),
+    "OFF": ("sbuf", [128, 8], U), "DD": ("sbuf", [128, 128], F), "WW": ("sbuf", [128, 1056], F),
+    "TT": ("sbuf", [128, 448], F), "XX": ("sbuf", [128, 32], F), "ZZ": ("sbuf", [128, 80], F),
+    "RM": ("sbuf", [128, 80], F), "SC": ("sbuf", [128, 80], F), "S2": ("sbuf", [128, 80], F),
+    "LT": ("sbuf", [128, 40], U), "LP": ("sbuf", [128, 16], U),
+    "QM": ("sbuf", [128, 4], F), "QX": ("sbuf", [128, 4], F), "QS": ("sbuf", [128, 4], F),
+    "RK": ("sbuf", [128, 8 * N], U), "QV": ("sbuf", [128, 4 * N], F), "RN": ("sbuf", [128, 4 * N], F), "PX": ("sbuf", [128, 4 * N], F),
+    "ZT": ("sbuf", [128, 32], F), "EX": ("sbuf", [128, 128], F), "ET": ("sbuf", [128, 128], F), "D2": ("sbuf", [128, 128], F),
+    "LQ": ("sbuf", [128, 64], F), "LA": ("sbuf", [128, 32], F), "LB": ("sbuf", [128, 32], F),
+    "CG": ("sbuf", [128, 4 * K], B), "RC": ("sbuf", [128, N * K], C8), "RP": ("sbuf", [128, N * K], P8),
+    "DF": ("sbuf", [128, 4 * K], F), "ER": ("sbuf", [128, 2048], F), "Y": ("sbuf", [128, 4 * W], F), "TM": ("sbuf", [128, 2 * K], F),
+    "PL": ("sbuf", [128, 16 * N], U), "LL": ("sbuf", [128, 32], U), "AC": ("sbuf", [128, 2048], F), "IO": ("sbuf", [128, 512], F),
+    "NB": ("sbuf", [128, 256], F), "ND": ("dram", [N, 128, 2], F), "SO": ("sbuf", [128, K], F),
+    "VI": ("sbuf", [128, 32], I), "VJ": ("sbuf", [128, 32], I), "UL": ("sbuf", [128, 32], U),
+    "V2": ("sbuf", [128, 2], I), "CI": ("sbuf", [128, 18], I), "CF": ("sbuf", [128, 64], F),
+    "SE": ("sbuf", [128, 4], U), "SD": ("sbuf", [128, 8], U), "D0": ("sbuf", [128, 128], F), "R0": ("sbuf", [128, 80], F),
+    "R1": ("sbuf", [128, 24], F), "D8": ("sbuf", [128, 8], F),
+}
+_EV = ["v", "a", "t", "ld_u", "ld_g0", "ld_g1", "on", "ul", "io1", "io2", "io3", "io4", "io5", "io6", "io7", "mst", "ut", "uq",
+       "gq0", "gq1", "ms0", "ms1", "sr", "sco", "sg", "sl", "er0", "xx", "za", "lt", "zw", "zl", "eq", "rks", "px", "lq",
+       "ga", "lst", "qc", "df", "erx", "so", "nb", "nd", "ll", "st", "sent", "pls", "hp", "hc", "tm", "c0", "c1", "c2", "c3"]
+SEMAPHORES = _EV + ["%s%d" % (e, n) for e in ("mm", "vc", "li", "rk", "ar", "pl") for n in range(N)] \
+    + ["%s%d" % (e, n) for e in ("fv", "fa") for n in range(4)]
+
+
+def tracked(q, T, name):
+    tot, pend = {}, {}
+
+    def rec(ins, ev=None):
+        e = ev or name
+        ins.then_inc(T.sem[e], 1)
+        tot[e] = tot.get(e, 0) + 1
+        pend[e] = tot[e]
+
+    def sync():
+        for e in list(pend):
+            q.wait_ge(T.sem[e], pend[e])
+        pend.clear()
+        return dict(tot)
+    return rec, sync
+
+
+def plan(T, topo, r):
+    core = T.cores[r]
+    others = [T.cores[(r - d) % N] for d in range(1, N)]
+    hs = [c for c in topo.cores_of(core) if c != core and all(topo.may_write(c, d) for d in others)]
+    hs.sort(key=lambda c: topo.die(c) == topo.die(core))
+    out, i = [], 0
+    for c, n in zip([core] + hs, SHARE[r]):
+        if n or c == core:
+            out.append((c, others[i:i + n]))
+        i += n
+    return others, out
+
+
+def transfer(topo, src, cores, mask, sem):
+    ids = [DstId(rid=topo.addr(d)[0], pnc=topo.addr(d)[1]) for d in cores]
+    return RemoteDMATransfer(dst_ids=ids, dma_engine_mask=mask, remote_sem=sem, srcs=[src], dsts=[src] * len(cores))
+
+
+def helper_program(g, core, T, topo):
+    S = T.sem
+    for r in range(N):
+        if topo.chip(T.cores[r]) != topo.chip(core):
+            continue
+        for c, dests in plan(T, topo, r)[1]:
+            if c != core:
+                continue
+            own = slice(K * r, K * r + K)
+            mask, ne = topo.mask(core, dests[0]), len(topo.engines(core, dests[0]))
+            nin = len(topo.engines(T.cores[r], core)) - len(topo.engines(T.cores[r], dests[0]))
+            for sem, src in (("hp", T.RP[:, own]), ("hc", T.RC[:, own].bitcast(dt.uint8))):
+                g.wait_ge(S[sem], nin)
+                g.remote_dma_fused([transfer(topo, src, dests, mask, S["ar%d" % r])], local_sem=S.sent)
+            g.wait_ge(S.sent, 2 * ne)
+
+
+def rank_program(g, core, T, topo):
+    r = T.rank_of(core)
+    if r is None:
+        return helper_program(g, core, T, topo)
+    A, AF = AluOpType, ActivationFunctionType
+    v, a, t, sy = g.vector, g.scalar, g.tensor, g.sync
+    S = T.sem
+    vr, vsync = tracked(v, T, "v")
+    ar, async_ = tracked(a, T, "a")
+    order = [r] + [s for s in range(N) if s != r]
+    turn = {s: n for n, s in enumerate(order)}
+
+    def ts(out, in0, s1, s2, op0, op1=None, ev=None):
+        if op1 is None:
+            vr(v.tensor_scalar(out, in0, s1, None, op0), ev)
+        else:
+            vr(v.tensor_scalar(out, in0, s1, s2, op0, op1), ev)
+
+    def tt(out, x, y, op, ev=None):
+        vr(v.tensor_tensor(out, x, y, op), ev)
+
+    def iota(out, pattern, base, ev):
+        g.iota(out, pattern, base, 0, allow_small_or_imprecise_dtypes=True).then_inc(S[ev], 1)
+
+    sy.dma_start(T.U4[:, 0:4], T.u[:, 0:4]).then_inc(S.ld_u, 16)
+    sy.dma_start(T.GR[:, 0:1024], T.gr[:, 0:1024]).then_inc(S.ld_g0, 16)
+    a.dma_start(T.GR[:, 1024:2048], T.gr[:, 1024:2048]).then_inc(S.ld_g1, 16)
+
+    g.iota(T.VI[:], [[0, 32]], 0, 1).then_inc(S.io1, 1)
+    g.iota(T.V2[:], [[128, 2]], 0, 1).then_inc(S.io2, 1)
+    iota(T.D0[:], [[0, 2], [128, 4], [1, 16]], 0, "io3")
+    iota(T.R0[:], [[0, 10], [1, 8]], 0, "io4")
+    g.wait_ge(S.on, 1)
+    g.affine_select(T.MM[:], T.ON[:, 0:516], [[-1, 516]], A.is_equal, 0.0, 3, 4).then_inc(S.mst, 1)
+    iota(T.R1[:], [[0, 4], [1, N]], 0, "io5")
+    iota(T.D8[:], [[0, 2], [32, 4]], 0, "io7")
+    g.wait_ge(S.sr, 2)
+    g.affine_select(T.SL[:], T.SR[:], [[0, 4], [-1, 128]], A.is_gt, -1.0, 0, 1).then_inc(S.sl, 1)
+    iota(T.IO[:], [[1, 512]], 0, "io6")
+
+    a.wait_ge(S.on, 1)
+    for out, n, ev in ((T.WW[:, 0:160], 160, "zw"), (T.WW[:, 512:704], 192, "zw"), (T.TT[:, 352:448], 96, "zw"),
+                       (T.ZT[:], 32, "zl"), (T.LQ[:, 16:32], 16, "zl")):
+        ar(a.activation(out, T.ON[:, 0:n], AF.Copy, scale=0.0), ev)
+    for b in range(4):
+        ar(a.activation(T.Y[:, W * b:W * b + 8], T.ON[:, 0:8], AF.Copy, scale=0.0), "zl")
+    a.wait_ge(S.ld_u, 16)
+    a.wait_ge(S.ul, 1)
+    ar(a.activation(T.UT[:], T.U4[:, 0:4].indirect(T.UL[:, 0:32]), AF.Copy), "ut")
+
+    vr(v.memset(T.ON[:], 1.0), "on")
+    v.wait_ge(S.io1, 1)
+    ts(T.VJ[:], T.VI[:], 3, None, A.bitwise_and)
+    vsync()
+    vr(v.tensor_copy(T.UL[:], T.VJ[:]), "ul")
+    v.wait_ge(S.io2, 1)
+    ci = lambda k: T.CI[:, 2 * k:2 * k + 2]
+    cf = lambda k: T.CF[:, 2 * k:2 * k + 2]
+    ts(ci(0), T.V2[:], 14, None, A.bitwise_and)
+    ts(ci(1), T.V2[:], 12, None, A.bitwise_and)
+    ts(ci(2), T.V2[:], 1, None, A.bitwise_and)
+    ts(ci(3), T.V2[:], 1, 1, A.arith_shift_right, A.bitwise_and)
+    ts(ci(4), T.V2[:], 4, 1, A.arith_shift_right, A.bitwise_and)
+    ts(ci(5), T.V2[:], 128, None, A.bitwise_and)
+    ts(ci(6), T.V2[:], 31, None, A.bitwise_and)
+    ts(ci(7), T.V2[:], 112, None, A.bitwise_and)
+    vsync()
+    vr(v.tensor_copy(T.CF[:, 0:16], T.CI[:, 0:16]))
+    vsync()
+    tt(cf(8), cf(3), cf(4), A.mult)
+    ts(cf(11), cf(1), 8.0, None, A.mult)
+    ts(cf(12), cf(2), 16.0, None, A.mult)
+    ts(cf(13), cf(3), 192.0, None, A.mult)
+    ts(cf(14), cf(4), 160.0, None, A.mult)
+    v.wait_ge(S.io3, 1)
+    ts(T.DD[:], T.D0[:], T.CF[:, 14:15], None, A.add)
+    v.wait_ge(S.io4, 1)
+    ts(T.RM[:], T.R0[:], 1.0, None, A.min)
+    vsync()
+    ts(cf(15), cf(8), 352.0, None, A.mult)
+    tt(cf(25), cf(5), cf(11), A.add)
+    tt(cf(26), cf(12), cf(13), A.add)
+    vsync()
+    tt(cf(27), cf(14), cf(15), A.subtract)
+    tt(cf(28), cf(25), cf(26), A.add)
+    vsync()
+    tt(T.SE[:, 0:2], cf(28), cf(27), A.add)
+
+    v.wait_ge(S.ut, 1)
+    vr(v.quantize_mx(T.UQ[:], T.UP[:], T.UT[:]), "uq")
+    for h in range(2):
+        v.wait_ge(S["ld_g%d" % h], 16)
+        c = slice(256 * h, 256 * h + 256)
+        vr(v.quantize_mx(T.GQ[:, c], T.GP[:, c], T.GR[:, 1024 * h:1024 * h + 1024]), "gq%d" % h)
+    v.wait_ge(S.mst, 1)
+    for b in range(4):
+        vr(v.quantize_mx(T.EQ[:, 128 * b:128 * b + 128], T.EP[:, 128 * b:128 * b + 128], T.MM[:, 3 - b:515 - b]), "eq")
+    t.wait_ge(S.uq, 1)
+    for h in range(2):
+        t.wait_ge(S["gq%d" % h], 1)
+        c = slice(256 * h, 256 * h + 256)
+        t.matmul_mx(T.PS[:, 512 * h:512 * h + 256], T.UQ[:], T.UP[:], T.GQ[:, c], T.GP[:, c], True, True).then_inc(S["ms%d" % h], 1)
+    for b in range(4):
+        c = slice(128 * b, 128 * b + 128)
+        t.matmul_mx(T.PS[:, 2048 + 512 * b:2176 + 512 * b], T.GQ[:, c], T.GP[:, c], T.UQ[:], T.UP[:], True, True).then_inc(S.t, 1)
+    for h in range(2):
+        a.wait_ge(S["ms%d" % h], 1)
+        ar(a.activation(T.SR[:, 256 * h:256 * h + 256], T.PS[:, 512 * h:512 * h + 256], AF.Abs), "sr")
+    a.wait_ge(S.t, 4)
+    ar(a.activation(T.SCO[:], T.PS[:, 2048:4096:512], AF.Abs), "sco")
+    async_()
+    ar(a.activation(T.SN[:], T.SCO[:], AF.Copy, scale=-1.0))
+    async_()
+    for b in (2, 3):
+        ar(a.activation(T.SG[:, 512 * b - 1024:512 * b - 512], T.SR[:], AF.Sign, bias=T.SN[:, b:b + 1]), "sg")
+    for k in range(4):
+        ar(a.activation(T.ER[:, 512 * k:512 * k + 512], T.GR[:, 512 * k:512 * k + 512], AF.Copy), "er0")
+
+    v.wait_ge(S.sr, 2)
+    v.wait_ge(S.sco, 1)
+
+    def before(b):
+        z = 640 * b
+        s, x = (T.SCO[:, b:b + 1], lambda i, j: T.SR[:, i:j]) if b < 2 else (0.0, lambda i, j: T.SG[:, 512 * b - 1024 + i:512 * b - 1024 + j])
+        if b:
+            ts(T.CM[:, z:z + 128 * b], x(0, 128 * b), s, None, A.is_ge)
+        ts(T.CM[:, z + 128 * b:z + 512], x(128 * b, 512), s, None, A.is_gt)
+
+    def equal(b):
+        ts(T.CM[:, 640 * b + 512:640 * b + 640], T.SL[:, 128 * b:128 * b + 128], T.SCO[:, b:b + 1], None, A.is_equal)
+
+    def count(b):
+        z = 640 * b
+        vr(v.tensor_tensor_scan(T.CN[:, 320 * b:320 * b + 320], T.CM[:, z:z + 320], T.CM[:, z + 320:z + 640], -256.0, A.add, A.add))
+    before(0)
+    before(1)
+    v.wait_ge(S.sl, 1)
+    for b in range(4):
+        equal(b)
+    v.wait_ge(S.sg, 2)
+    before(2)
+    vsync()
+    before(3)
+    for b in range(3):
+        count(b)
+    vsync()
+    count(3)
+    vsync()
+
+    def permute(val, out, between=None):
+        vr(v.tensor_copy(T.WW[:, 0:1056].indirect(T.OFF[:, 0:8]), val))
+        vsync()
+        if between:
+            between()
+        vr(v.transpose(T.TT[:, 0:160], T.WW[:, 0:160]))
+        vr(v.transpose(T.TT[:, 160:352], T.WW[:, 512:704]))
+        vsync()
+        vr(v.tensor_copy(T.XX[:], T.TT[:, 0:448].indirect(T.SE[:, 0:2])), "xx")
+        n = vsync()["xx"]
+        a.wait_ge(S.xx, n)
+        vr(v.tensor_copy(T.ZZ[:, 0:80:4], T.XX[:, 0:20]))
+        for p in (0, 64):
+            vr(v.tensor_copy(T.ZZ[64 - p:128 - p, 2:80:4], T.XX[p:p + 64, 0:20]))
+        for d in (1, 3):
+            for p in range(4):
+                o = 32 * (p ^ d)
+                dst, src = T.ZZ[o:o + 32, d:80:4], T.XX[32 * p:32 * p + 32, 0:20]
+                if d == 1 and p < 3:
+                    vr(v.tensor_copy(dst, src))
+                else:
+                    ar(a.activation(dst, src, AF.Copy), "za")
+        vsync()
+        v.wait_ge(S.za, 5 * n)
+        vr(v.tensor_tensor_scan(out[:], T.RM[:], T.ZZ[:], 0.0, A.mult, A.add))
+        vsync()
+        return out[:, 7:80:8]
+
+    rk = T.CN[:, 319:1280:320]
+    ts(T.OFF[:, 0:4], rk, 256.0, None, A.add)
+    ts(T.OFF[:, 4:8], rk, 784.0, None, A.add)
+    ts(T.QM[:], rk, -96.0, None, A.is_lt)
+    ts(T.QX[:], rk, float(264 + K * r), None, A.add)
+    vsync()
+    v.wait_ge(S.zw, 3)
+    tt(T.QS[:], T.QM[:], T.QX[:], A.mult)
+    num = permute(T.DD[:], T.SC, lambda: ts(T.RK[:, 8 * r:8 * r + 4], T.QS[:], 0.0, None, A.add, ev="rks"))
+    for k in (2, 3, 0, 1):
+        ts(T.LT[:, L * k:L * k + L], num, 4.0, float(k), A.mult, A.add, ev="lt" if k > 1 else None)
+
+    a.wait_ge(S.lt, 2)
+    for k in (2, 3):
+        ar(a.activation(T.CG[:, k:4 * K:4], T.GR[:].indirect(T.LT[:, L * k:L * k + L]), AF.Copy), "ga")
+    vsync()
+    for k in (0, 1):
+        vr(v.tensor_copy(T.CG[:, k:4 * K:4], T.GR[:].indirect(T.LT[:, L * k:L * k + L])))
+    vsync()
+    v.wait_ge(S.ga, 2)
+    own = slice(K * r, K * r + K)
+    vr(v.quantize_mx(T.RC[:, own], T.RP[:, own], T.CG[:]), "qc")
+    ts(T.LP[:, 0:L], num, 0.0, None, A.add, ev="lst")
+    ts(T.LP[:, L:16], T.SC[:, 7:55:8], 0.0, None, A.add, ev="lst")
+
+    others, roads = plan(T, topo, r)
+    off, ne = topo.mask(core, others[0]), len(topo.engines(core, others[0]))
+    hs = [c for c, _ in roads[1:]]
+    on = topo.mask(core, hs[0]) & ~off if hs else 0
+    n_on = len(topo.engines(core, hs[0])) - ne if hs else 0
+    direct = roads[0][1]
+    sent = [0]
+
+    def send(trs, n):
+        g.remote_dma_fused(trs, local_sem=S.sent)
+        sent[0] += n
+
+    def out(src, sem, hsem):
+        trs = []
+        if hs:
+            trs.append(transfer(topo, src, hs, on, S[hsem]))
+        if direct:
+            trs.append(transfer(topo, src, direct, off, S[sem]))
+        send(trs, (n_on if hs else 0) + (ne if direct else 0))
+    g.wait_ge(S.rks, 1)
+    send([transfer(topo, T.RK[:, 8 * r:8 * r + 4], others, off, S["rk%d" % r])], ne)
+    g.wait_ge(S.qc, 1)
+    out(T.RP[:, own], "ar%d" % r, "hp")
+    out(T.RC[:, own].bitcast(dt.uint8), "ar%d" % r, "hc")
+
+    mixed = lambda s: s not in (0, r)
+
+    def free(n):
+        t.wait_ge(S["vc%d" % n], 3 if mixed(order[n]) else 4)
+        if mixed(order[n]):
+            t.wait_ge(S.c3, order[n])
+
+    def decode(n):
+        s = order[n]
+        if n == 0:
+            t.wait_ge(S.qc, 1)
+            t.wait_ge(S.eq, 4)
+            t.wait_ge(S.sr, 2)
+        else:
+            t.wait_ge(S["ar%d" % s], 2 * ne)
+            if n == 1:
+                t.wait_ge(S.sco, 1)
+            else:
+                free(n - 2)
+        z = 2048 * (n % 2)
+        for b in range(4):
+            t.matmul_mx(T.PS[:, z + 512 * b:z + 512 * b + K], T.EQ[:, 128 * b:128 * b + 128], T.EP[:, 128 * b:128 * b + 128],
+                        T.RC[:, K * s:K * s + K], T.RP[:, K * s:K * s + K], True, True).then_inc(S["mm%d" % n], 1)
+
+    def unload(n):
+        s, z = order[n], 2048 * (n % 2)
+        a.wait_ge(S["mm%d" % n], 4)
+        for b in range(3 if mixed(s) else 4):
+            o = W * b + 8 + K * s
+            ar(a.activation(T.Y[:, o:o + K], T.PS[:, z + 512 * b:z + 512 * b + K], AF.Copy), "vc%d" % n)
+    for n in range(N):
+        decode(n)
+
+    a.wait_ge(S.io6, 1)
+    a.wait_ge(S.lst, 2)
+    ar(a.activation(T.NB[:], T.IO[:].indirect(T.LP[:]), AF.Copy), "nb")
+    ar(a.activation(T.SO[:], T.SR[:].indirect(T.LP[:, 0:L]), AF.Copy), "so")
+
+    ts(cf(9), cf(2), T.CF[:, 8:9], None, A.mult)
+    ts(cf(16), cf(0), 0.5, None, A.mult)
+    ts(cf(17), cf(5), 0.0625, None, A.mult)
+    tt(cf(18), cf(2), cf(4), A.add)
+    v.wait_ge(S.io5, 1)
+    ts(T.RN[:], T.R1[:], 1.0, None, A.min)
+    v.wait_ge(S.io7, 1)
+    ts(T.SD[:], T.D8[:], T.CF[:, 12:13], None, A.add)
+    vsync()
+    ts(cf(19), cf(9), 64.0, None, A.mult)
+    ts(cf(20), cf(18), 32.0, None, A.mult)
+    tt(cf(21), cf(16), cf(17), A.add)
+    vsync()
+    tt(cf(22), cf(20), cf(19), A.subtract)
+    vsync()
+    tt(T.SE[:, 2:4], cf(21), cf(22), A.add)
+
+    v.wait_ge(S.mm0, 4)
+    for b in range(4):
+        tt(T.DF[:, K * b:K * b + K], T.CG[:, b:4 * K:4], T.PS[:, 512 * b:512 * b + K], A.subtract, ev="df")
+    a.wait_ge(S.df, 4)
+    unload(0)
+
+    for s in order[1:]:
+        v.wait_ge(S["rk%d" % s], ne)
+    for b in range(4):
+        vr(v.tensor_copy(T.QV[:, N * b:N * b + N], T.RK[:, b:8 * N:8]))
+    vsync()
+    vr(v.tensor_tensor_scan(T.PX[:], T.RN[:], T.QV[:], 0.0, A.mult, A.max), "px")
+    vsync()
+    v.wait_ge(S.zl, 6)
+    pl = lambda s: T.PL[:, 16 * s:16 * s + L]
+    if r:
+        for b in range(4):
+            c = N * b + r - 1
+            ts(T.EX[:, 32 * b:32 * b + 32], T.ZT[:], T.PX[:, c:c + 1], None, A.add)
+        vsync()
+        vr(v.transpose(T.ET[:], T.EX[:]))
+        vsync()
+        vr(v.tensor_copy(T.D2[:], T.ET[:].indirect(T.SD[:, 0:8])))
+        vsync()
+        ts(pl(r), permute(T.D2[:], T.S2), 0.0, None, A.add, ev="pls")
+        g.wait_ge(S.pls, 1)
+        send([transfer(topo, pl(r), others, off, S["pl%d" % r])], ne)
+    g.wait_ge(S.nd, 16)
+    send([transfer(topo, T.ND[r], others, off, S["li%d" % r])], ne)
+    a.wait_ge(S.px, 1)
+    for p in range(4):
+        for d in range(4):
+            ar(a.activation(T.LQ[32 * d:32 * d + 32, p:16:4], T.PX[32 * p:32 * p + 32, N - 1:4 * N:N], AF.Copy), "lq")
+
+    vsync()
+    v.wait_ge(S.er0, 4)
+    vr(v.tensor_copy(T.ER[:].indirect(T.LT[:, 0:40]), T.DF[:]), "erx")
+    v.wait_ge(S.lq, 16)
+    vr(v.transpose(T.LA[:], T.LQ[:, 0:32]))
+    vsync()
+    vr(v.tensor_copy(T.LB[:, 0:16], T.LA[:, 16:32]))
+    vr(v.tensor_copy(T.LB[:, 16:32], T.LA[:, 0:16]))
+    vsync()
+    vr(v.transpose(T.LQ[:, 32:64], T.LB[:]))
+    vsync()
+    vr(v.tensor_copy(T.LL[:], T.LQ[:].indirect(T.SE[:, 2:4])), "ll")
+    vsync()
+
+    tm = lambda s: T.TM[:, K * (s % 2):K * (s % 2) + K]
+    for n in range(1, N):
+        s = order[n]
+        unload(n)
+        if mixed(s):
+            if s == 1 or (s == 2 and r == 1):
+                async_()
+            a.wait_ge(S["pl%d" % s], ne)
+            if s > 1:
+                a.wait_ge(S.c3, s - 1)
+            ar(a.activation(tm(s), T.Y[:, 3 * W:3 * W + 8 + K * s].indirect(pl(s)), AF.Copy), "tm")
+    nt = 0
+    for s in range(1, N):
+        if s != r:
+            v.wait_ge(S["pl%d" % s], ne)
+        for k in ([0, 1] if s == 1 else [s]):
+            v.wait_ge(S["vc%d" % turn[k]], 3 if mixed(k) else 4)
+        for b in (3, 0, 1, 2):
+            o = W * b + 8 + K * s
+            if s > 1:
+                v.wait_ge(S["c%d" % b], s - 1)
+            if b == 3 and mixed(s):
+                nt += 1
+                v.wait_ge(S.tm, nt)
+                z = 2048 * (turn[s] % 2) + 512 * b
+                tt(T.Y[:, o:o + K], tm(s), T.PS[:, z:z + K], A.add, ev="c3")
+            else:
+                tt(T.Y[:, o:o + K], T.Y[:, W * b:o].indirect(pl(s)), T.Y[:, o:o + K], A.add, ev="c%d" % b)
+
+    def lay(b, h):
+        return T.AC[:, 512 * h + b:512 * h + 512:4], T.Y[:, W * b:W * b + W].indirect(T.LL[:, 8 * h:8 * h + 8])
+
+    def lay_a(b, h):
+        dst, win = lay(b, h)
+        ar(a.activation(dst, win, AF.Copy), "fa%d" % h)
+    a.wait_ge(S.ll, 1)
+    a.wait_ge(S.c3, N - 1)
+    for h in range(4):
+        lay_a(3, h)
+    a.wait_ge(S.c2, N - 1)
+    a.wait_ge(S.c1, N - 1)
+    v.wait_ge(S.c0, N - 1)
+    for h in range(4):
+        for b in ((0, 1) if h < 2 else (0,)):
+            if h == 0 and b == 1:
+                v.wait_ge(S.c1, N - 1)
+            dst, win = lay(b, h)
+            vr(v.tensor_copy(dst, win), "fv%d" % h)
+        for b in ((2,) if h < 2 else (2, 1)):
+            lay_a(b, h)
+    vsync()
+
+    sy.wait_ge(S.nb, 1)
+    sy.dma_start(T.ND[r], T.NB[0:1, :]).then_inc(S.nd, 16)
+    sy.dma_start(T.nb[r:r + 1, :], T.NB[0:1, 0:K]).then_inc(S.st, 16)
+    sy.wait_ge(S.so, 1)
+    sy.dma_start(T.sc[:], T.SO[0:1, :]).then_inc(S.st, 16)
+    sy.wait_ge(S.erx, 1)
+    sy.dma_start(T.er[:], T.ER[:]).then_inc(S.st, 16)
+    for s in order[1:]:
+        sy.wait_ge(S["li%d" % s], ne)
+        sy.dma_start(T.nb[s:s + 1, :], T.ND[s, 0:K // 2, :]).then_inc(S.st, 16)
+    for h in range(4):
+        sy.wait_ge(S["fv%d" % h], 2 if h < 2 else 1)
+        sy.wait_ge(S["fa%d" % h], 2 if h < 2 else 3)
+        sy.dma_start(T.acc[:, 512 * h:512 * h + 512], T.AC[:, 512 * h:512 * h + 512]).then_inc(S.st, 16)
+    g.wait_ge(S.sent, sent[0])
+    sy.wait_ge(S.st, 16 * (N + 6))

@@ -4,40 +4,43 @@ from concourse.mybir import dt, AluOpType, ActivationFunctionType
 N, TC, K = 6, 512, 160
 W = 8 + N * K
 L = K // 16
-SHARE = [(3, 1, 1)] + [(2, 2, 1)] * (N - 1)
+SHARE = [(3, 1, 1)] * N
+MIXED = (3, 2)
+PLAIN = (0, 1)
 
 F, B, I, U, C8, P8 = "float32", "bfloat16", "int32", "uint16", "float8_e4m3fn_x4", "uint8"
 SCRATCH = {
     "U4": ("sbuf", [128, 16], B), "UT": ("sbuf", [128, 512], B),
     "UQ": ("sbuf", [128, 128], C8), "UP": ("sbuf", [128, 128], P8),
     "GR": ("sbuf", [128, 2048], B), "GQ": ("sbuf", [128, 512], C8), "GP": ("sbuf", [128, 512], P8),
-    "ON": ("sbuf", [128, 640], B), "MM": ("sbuf", [128, 516], B),
+    "ON": ("sbuf", [128, 516], B), "MM": ("sbuf", [128, 516], B),
     "EQ": ("sbuf", [128, 512], C8), "EP": ("sbuf", [128, 512], P8),
     "PS": ("psum", [128, 4096], F),
-    "SR": ("sbuf", [128, 512], F), "SL": ("sbuf", [128, 512], F), "SCO": ("sbuf", [128, 4], F), "SN": ("sbuf", [128, 4], F),
-    "SG": ("sbuf", [128, 1024], B), "CM": ("sbuf", [128, 2560], B), "CN": ("sbuf", [128, 1280], B),
-    "OFF": ("sbuf", [128, 8], U), "DD": ("sbuf", [128, 128], F), "WW": ("sbuf", [128, 1056], F),
+    "SR": ("sbuf", [128, 512], F), "SL": ("sbuf", [128, 512], F), "SCO": ("sbuf", [128, 4], F), "AS": ("sbuf", [128, 2], F),
+    "HB": ("sbuf", [128, 2], F), "SG": ("sbuf", [128, 768], B), "CM": ("sbuf", [128, 1800], B), "CN": ("sbuf", [128, 1280], B),
+    "OFF": ("sbuf", [128, 8], U), "DD": ("sbuf", [128, 64], F), "WW": ("sbuf", [128, 1072], F),
     "TT": ("sbuf", [128, 448], F), "XX": ("sbuf", [128, 32], F), "ZZ": ("sbuf", [128, 80], F),
-    "RM": ("sbuf", [128, 80], F), "SC": ("sbuf", [128, 80], F), "S2": ("sbuf", [128, 80], F),
+    "RM": ("sbuf", [128, 80], F), "SC": ("sbuf", [128, 80], F),
     "LT": ("sbuf", [128, 40], U), "LP": ("sbuf", [128, 16], U),
-    "QM": ("sbuf", [128, 4], F), "QX": ("sbuf", [128, 4], F), "QS": ("sbuf", [128, 4], F),
-    "RK": ("sbuf", [128, 8 * N], U), "QV": ("sbuf", [128, 4 * N], F), "RN": ("sbuf", [128, 4 * N], F), "PX": ("sbuf", [128, 4 * N], F),
-    "ZT": ("sbuf", [128, 32], F), "EX": ("sbuf", [128, 128], F), "ET": ("sbuf", [128, 128], F), "D2": ("sbuf", [128, 128], F),
-    "LQ": ("sbuf", [128, 64], F), "LA": ("sbuf", [128, 32], F), "LB": ("sbuf", [128, 32], F),
+    "RO": ("sbuf", [128, 8], B), "RK": ("sbuf", [128, 64], B), "RL": ("sbuf", [128, 4], U), "BA": ("sbuf", [128, 64], F),
+    "Q0": ("sbuf", [128, 64], F), "Q1": ("sbuf", [128, 64], F), "OP": ("sbuf", [128, 4], F),
+    "EX": ("sbuf", [128, 128], F), "ET": ("sbuf", [128, 128], F),
+    "LQ": ("sbuf", [128, 64], F), "LA": ("sbuf", [128, 64], F), "LF": ("sbuf", [128, 32], F),
     "CG": ("sbuf", [128, 4 * K], B), "RC": ("sbuf", [128, N * K], C8), "RP": ("sbuf", [128, N * K], P8),
-    "DF": ("sbuf", [128, 4 * K], F), "ER": ("sbuf", [128, 2048], F), "Y": ("sbuf", [128, 4 * W], F), "TM": ("sbuf", [128, 2 * K], F),
+    "DF": ("sbuf", [128, 4 * K], F), "ER": ("sbuf", [128, 2048], F), "Y": ("sbuf", [128, 4 * W], F), "TM": ("sbuf", [128, 4 * K], F),
     "PL": ("sbuf", [128, 16 * N], U), "LL": ("sbuf", [128, 32], U), "AC": ("sbuf", [128, 2048], F), "IO": ("sbuf", [128, 512], F),
     "NB": ("sbuf", [128, 256], F), "ND": ("dram", [N, 128, 2], F), "SO": ("sbuf", [128, K], F),
-    "VI": ("sbuf", [128, 32], I), "VJ": ("sbuf", [128, 32], I), "UL": ("sbuf", [128, 32], U),
-    "V2": ("sbuf", [128, 2], I), "CI": ("sbuf", [128, 18], I), "CF": ("sbuf", [128, 64], F),
-    "SE": ("sbuf", [128, 4], U), "SD": ("sbuf", [128, 8], U), "D0": ("sbuf", [128, 128], F), "R0": ("sbuf", [128, 80], F),
-    "R1": ("sbuf", [128, 24], F), "D8": ("sbuf", [128, 8], F),
+    "VI": ("sbuf", [128, 32], I), "VJ": ("sbuf", [128, 32], I), "VK": ("sbuf", [128, 2], I), "UL": ("sbuf", [128, 32], U),
+    "CF": ("sbuf", [128, 2], F), "SE": ("sbuf", [128, 2], U), "D0": ("sbuf", [128, 64], F),
+    "TA": ("sbuf", [128, 32], F), "TB": ("sbuf", [128, 32], F),
 }
-_EV = ["v", "a", "t", "ld_u", "ld_g0", "ld_g1", "on", "ul", "io1", "io2", "io3", "io4", "io5", "io6", "io7", "mst", "ut", "uq",
-       "gq0", "gq1", "ms0", "ms1", "sr", "sco", "sg", "sl", "er0", "xx", "za", "lt", "zw", "zl", "eq", "rks", "px", "lq",
-       "ga", "lst", "qc", "df", "erx", "so", "nb", "nd", "ll", "st", "sent", "pls", "hp", "hc", "tm", "c0", "c1", "c2", "c3"]
-SEMAPHORES = _EV + ["%s%d" % (e, n) for e in ("mm", "vc", "li", "rk", "ar", "pl") for n in range(N)] \
-    + ["%s%d" % (e, n) for e in ("fv", "fa") for n in range(4)]
+_EV = ["v", "a", "mc", "ld_u", "on", "ul", "io1", "io2", "io3", "io4", "mst", "ut", "uq", "sco", "cnt", "sl", "er0", "xx", "za", "lt",
+       "eq", "rks", "px", "lq", "ga", "lst", "qc", "df", "erx", "so", "nb", "nd", "ll", "st", "sent", "hp", "hc", "hl", "rk", "mo",
+       "zy", "sr", "u0", "left"]
+SEMAPHORES = _EV + ["%s%d" % (e, n) for e in ("li", "ar", "pl") for n in range(N)] \
+    + ["%s%d" % (e, n) for e in ("ld", "gq", "ms", "fv", "fa", "c", "tm", "mm", "un") for n in range(4)]
+
+A, AF = AluOpType, ActivationFunctionType
 
 
 def tracked(q, T, name):
@@ -53,56 +56,13 @@ def tracked(q, T, name):
         for e in list(pend):
             q.wait_ge(T.sem[e], pend[e])
         pend.clear()
-        return dict(tot)
     return rec, sync
 
 
-def plan(T, topo, r):
-    core = T.cores[r]
-    others = [T.cores[(r - d) % N] for d in range(1, N)]
-    hs = [c for c in topo.cores_of(core) if c != core and all(topo.may_write(c, d) for d in others)]
-    hs.sort(key=lambda c: topo.die(c) == topo.die(core))
-    out, i = [], 0
-    for c, n in zip([core] + hs, SHARE[r]):
-        if n or c == core:
-            out.append((c, others[i:i + n]))
-        i += n
-    return others, out
-
-
-def transfer(topo, src, cores, mask, sem):
-    ids = [DstId(rid=topo.addr(d)[0], pnc=topo.addr(d)[1]) for d in cores]
-    return RemoteDMATransfer(dst_ids=ids, dma_engine_mask=mask, remote_sem=sem, srcs=[src], dsts=[src] * len(cores))
-
-
-def helper_program(g, core, T, topo):
-    S = T.sem
-    for r in range(N):
-        if topo.chip(T.cores[r]) != topo.chip(core):
-            continue
-        for c, dests in plan(T, topo, r)[1]:
-            if c != core:
-                continue
-            own = slice(K * r, K * r + K)
-            mask, ne = topo.mask(core, dests[0]), len(topo.engines(core, dests[0]))
-            nin = len(topo.engines(T.cores[r], core)) - len(topo.engines(T.cores[r], dests[0]))
-            for sem, src in (("hp", T.RP[:, own]), ("hc", T.RC[:, own].bitcast(dt.uint8))):
-                g.wait_ge(S[sem], nin)
-                g.remote_dma_fused([transfer(topo, src, dests, mask, S["ar%d" % r])], local_sem=S.sent)
-            g.wait_ge(S.sent, 2 * ne)
-
-
-def rank_program(g, core, T, topo):
-    r = T.rank_of(core)
-    if r is None:
-        return helper_program(g, core, T, topo)
-    A, AF = AluOpType, ActivationFunctionType
-    v, a, t, sy = g.vector, g.scalar, g.tensor, g.sync
-    S = T.sem
+def calls(g, T):
+    v, a = g.vector, g.scalar
     vr, vsync = tracked(v, T, "v")
     ar, async_ = tracked(a, T, "a")
-    order = [r] + [s for s in range(N) if s != r]
-    turn = {s: n for n, s in enumerate(order)}
 
     def ts(out, in0, s1, s2, op0, op1=None, ev=None):
         if op1 is None:
@@ -113,366 +73,413 @@ def rank_program(g, core, T, topo):
     def tt(out, x, y, op, ev=None):
         vr(v.tensor_tensor(out, x, y, op), ev)
 
-    def iota(out, pattern, base, ev):
-        g.iota(out, pattern, base, 0, allow_small_or_imprecise_dtypes=True).then_inc(S[ev], 1)
+    def cp(out, x, ev=None):
+        vr(v.tensor_copy(out, x), ev)
 
-    sy.dma_start(T.U4[:, 0:4], T.u[:, 0:4]).then_inc(S.ld_u, 16)
-    sy.dma_start(T.GR[:, 0:1024], T.gr[:, 0:1024]).then_inc(S.ld_g0, 16)
-    a.dma_start(T.GR[:, 1024:2048], T.gr[:, 1024:2048]).then_inc(S.ld_g1, 16)
+    def act(out, x, func=AF.Copy, ev=None, **kw):
+        ar(a.activation(out, x, func, **kw), ev)
+
+    def iota(out, pattern, base, ev):
+        g.iota(out, pattern, base, 0, allow_small_or_imprecise_dtypes=True).then_inc(T.sem[ev], 1)
+    return vr, vsync, async_, ts, tt, cp, act, iota
+
+
+def plan(T, topo, r):
+    core = T.cores[r]
+    others = [T.cores[(r - d) % N] for d in range(1, N)]
+    hs = [c for c in topo.cores_of(core) if c != core and all(topo.may_write(c, d) for d in others)]
+    hs.sort(key=lambda c: topo.die(c) == topo.die(core))
+    out, i = [], 0
+    for c, n in zip([core] + hs, SHARE[r]):
+        out.append((c, others[i:i + n]))
+        i += n
+    return others, out
+
+
+def lister(T, topo, s):
+    return plan(T, topo, s)[1][-1][0]
+
+
+def transfer(topo, src, cores, mask, sem, dsts=None):
+    ids = [DstId(rid=topo.addr(d)[0], pnc=topo.addr(d)[1]) for d in cores]
+    return RemoteDMATransfer(dst_ids=ids, dma_engine_mask=mask, remote_sem=sem, srcs=[src], dsts=dsts or [src] * len(cores))
+
+
+def table(g, T, C, even, odd, step):
+    vr, vsync, async_, ts, tt, cp, act, iota = C
+    iota(T.TA[:, 0:16], even[0], even[1], "io2")
+    iota(T.TA[:, 16:32], odd[0], odd[1], "io2")
+
+    def finish():
+        g.vector.wait_ge(T.sem.io2, 2)
+        vr(g.vector.transpose(T.TB[:], T.TA[:]))
+        vsync()
+        ts(T.SE[:, 0:1], T.TB[:, 0:1], 0.0, None, A.add)
+        ts(T.SE[:, 1:2], T.TB[:, 0:1], float(step), None, A.add)
+    return finish
+
+
+def permute_tables(g, T, C, col):
+    vr = C[0]
+    fin = table(g, T, C, ([[32, 4], [192, 2], [16, 2]], col), ([[32, 4], [-160, 2], [16, 2]], 160 + col), 128)
+    v = g.vector
+    vr(v.memset(T.WW[:, 0:192], 0.0))
+    vr(v.memset(T.TT[:, 352:448], 0.0))
+    vr(v.memset(T.RM[:], 1.0))
+    C[1]()
+    vr(v.memset(T.RM[:, 0:80:8], 0.0))
+    return fin
+
+
+def permute(g, T, C, val, n):
+    vr, vsync, async_, ts, tt, cp, act, iota = C
+    v, a = g.vector, g.scalar
+    cp(T.WW[:].indirect(T.OFF[:, 0:n]), val)
+    vsync()
+    vr(v.transpose(T.TT[:, 0:160], T.WW[:, 16:176]))
+    vr(v.transpose(T.TT[:, 160:352], T.WW[:, 0:192]))
+    vsync()
+    cp(T.XX[:], T.TT[:].indirect(T.SE[:]), "xx")
+    vsync()
+    a.wait_ge(T.sem.xx, 1)
+    cp(T.ZZ[:, 0:80:4], T.XX[:, 0:20])
+    for p in (0, 64):
+        cp(T.ZZ[64 - p:128 - p, 2:80:4], T.XX[p:p + 64, 0:20])
+    for d in (1, 3):
+        for p in range(4):
+            o = 32 * (p ^ d)
+            dst, src = T.ZZ[o:o + 32, d:80:4], T.XX[32 * p:32 * p + 32, 0:20]
+            if d == 1 and p < 3:
+                cp(dst, src)
+            else:
+                act(dst, src, ev="za")
+    vsync()
+    v.wait_ge(T.sem.za, 5)
+    vr(v.tensor_tensor_scan(T.SC[:], T.RM[:], T.ZZ[:], 0.0, A.mult, A.add))
+    vsync()
+    return T.SC[:, 7:80:8]
+
+
+def make_list(g, T, s, ne):
+    C = calls(g, T)
+    vr, vsync, async_, ts, tt, cp, act, iota = C
+    v, a, S = g.vector, g.scalar, T.sem
+    m = s or N
+    g.iota(T.VI[:, 0:4], [[1, 4]], 0, 8).then_inc(S.io1, 1)
+    iota(T.BA[:], [[0, 8], [2 * K, 8]], 2 * 8 + TC - 2 * K, "io3")
+    if s:
+        fin = permute_tables(g, T, C, 14)
+    else:
+        fin = table(g, T, C, ([[1, 8], [32, 2]], 0), ([[1, 8], [-32, 2]], 32), 8)
+        vr(v.memset(T.LQ[:, 16:32], 0.0))
+    vr(v.memset(T.RK[:, 0:8], float(2 * K - 2 * 8 - TC)))
+    vr(v.memset(T.RK[:, 8 * m + 8:64], 0.0))
+    vr(v.memset(T.EX[:], 0.0))
+    v.wait_ge(S.io1, 1)
+    ts(T.VJ[:, 0:4], T.VI[:, 0:4], 63, None, A.bitwise_and)
+    ts(T.VK[:, 0:1], T.VI[:, 0:1], 128, None, A.bitwise_and)
+    vsync()
+    cp(T.RL[:], T.VJ[:, 0:4])
+    cp(T.CF[:, 0:1], T.VK[:, 0:1])
+    fin()
+    ts(T.OP[:, 0:1], T.CF[:, 0:1], 528 / 128, 272.0, A.mult, A.add)
+    ts(T.OP[:, 1:2], T.CF[:, 0:1], -528 / 128, 800.0, A.mult, A.add)
+    vsync()
+    v.wait_ge(S.io3, 1)
+    v.wait_ge(S.rk, ne * (m + 1 if s else m))
+    win = T.RK[:].indirect(T.RL[:])
+    tt(T.Q1[:], win, T.BA[:], A.add)
+    ts(T.Q0[:], win, float(2 * K - TC), 4096.0, A.is_lt, A.mult)
+    vsync()
+    vr(v.tensor_tensor_scan(T.EX[:, 0:128:2], T.Q0[:], T.Q1[:], 0.0, A.add, A.min), "px")
+    if s:
+        for h in range(2):
+            ts(T.OFF[:, h:8:2], T.RO[:, 0:4], 0.5, T.OP[:, h:h + 1], A.mult, A.add)
+        vsync()
+        vr(v.transpose(T.ET[:], T.EX[:]))
+        vsync()
+        out = T.PL[:, 16 * s:16 * s + L]
+        ts(out, permute(g, T, C, T.ET[:], 8), 0.5, None, A.mult, ev="hl")
+        vsync()
+        return out, "pl%d" % s
+    vsync()
+    a.wait_ge(S.px, 1)
+    for p in range(4):
+        for d in range(4):
+            dst, src = T.LQ[32 * d:32 * d + 32, p:16:4], T.EX[32 * p:32 * p + 32, 14:128:32]
+            if d < 2:
+                cp(dst, src)
+            else:
+                act(dst, src, ev="lq")
+    vsync()
+    v.wait_ge(S.lq, 8)
+    for h in range(2):
+        vr(v.transpose(T.LA[:, 32 * h:32 * h + 32], T.LQ[:, 0:32]))
+    vsync()
+    vr(v.transpose(T.LQ[:, 32:64], T.LA[:, 16:48]))
+    vsync()
+    ts(T.LF[:], T.LQ[:].indirect(T.SE[:]), 0.5, None, A.mult)
+    vsync()
+    cp(T.LL[:], T.LF[:], "hl")
+    vsync()
+    return T.LL[:], "ll"
+
+
+def helper_program(g, core, T, topo):
+    S = T.sem
+    for r in range(N):
+        if topo.chip(T.cores[r]) != topo.chip(core):
+            continue
+        others, roads = plan(T, topo, r)
+        mask, ne = topo.mask(core, others[0]), len(topo.engines(core, others[0]))
+        nin = len(topo.engines(T.cores[r], core)) - ne
+        own = slice(K * r, K * r + K)
+        mine = make_list(g, T, r, ne) if core == lister(T, topo, r) else None
+        for c, dests in roads:
+            if c != core:
+                continue
+            for sem, src in (("hp", T.RP[:, own]), ("hc", T.RC[:, own].bitcast(dt.uint8))):
+                g.wait_ge(S[sem], nin)
+                g.remote_dma_fused([transfer(topo, src, dests, mask, S["ar%d" % r])], local_sem=S.sent)
+            if mine:
+                g.wait_ge(S.hl, 1)
+                g.remote_dma_fused([transfer(topo, mine[0], others + [T.cores[r]], mask, S[mine[1]])], local_sem=S.sent)
+            g.wait_ge(S.sent, (3 if mine else 2) * ne)
+
+
+def rank_program(g, core, T, topo):
+    r = T.rank_of(core)
+    if r is None:
+        return helper_program(g, core, T, topo)
+    v, a, t, sy = g.vector, g.scalar, g.tensor, g.sync
+    S = T.sem
+    C = calls(g, T)
+    vr, vsync, async_, ts, tt, cp, act, iota = C
+    blk = lambda b: slice(128 * b, 128 * b + 128)
+    bank = lambda n, w: T.PS[:, 512 * n:512 * n + w]
+
+    a.dma_start(T.U4[:, 0:4], T.u[:, 0:4]).then_inc(S.ld_u, 16)
+    for q in range(4):
+        (a if q % 2 else sy).dma_start(T.GR[:, 512 * q:512 * q + 512], T.gr[:, 512 * q:512 * q + 512]).then_inc(S["ld%d" % q], 16)
 
     g.iota(T.VI[:], [[0, 32]], 0, 1).then_inc(S.io1, 1)
-    g.iota(T.V2[:], [[128, 2]], 0, 1).then_inc(S.io2, 1)
-    iota(T.D0[:], [[0, 2], [128, 4], [1, 16]], 0, "io3")
-    iota(T.R0[:], [[0, 10], [1, 8]], 0, "io4")
-    g.wait_ge(S.on, 1)
-    g.affine_select(T.MM[:], T.ON[:, 0:516], [[-1, 516]], A.is_equal, 0.0, 3, 4).then_inc(S.mst, 1)
-    iota(T.R1[:], [[0, 4], [1, N]], 0, "io5")
-    iota(T.D8[:], [[0, 2], [32, 4]], 0, "io7")
-    g.wait_ge(S.sr, 2)
-    g.affine_select(T.SL[:], T.SR[:], [[0, 4], [-1, 128]], A.is_gt, -1.0, 0, 1).then_inc(S.sl, 1)
-    iota(T.IO[:], [[1, 512]], 0, "io6")
-
-    a.wait_ge(S.on, 1)
-    for out, n, ev in ((T.WW[:, 0:160], 160, "zw"), (T.WW[:, 512:704], 192, "zw"), (T.TT[:, 352:448], 96, "zw"),
-                       (T.ZT[:], 32, "zl"), (T.LQ[:, 16:32], 16, "zl")):
-        ar(a.activation(out, T.ON[:, 0:n], AF.Copy, scale=0.0), ev)
-    for b in range(4):
-        ar(a.activation(T.Y[:, W * b:W * b + 8], T.ON[:, 0:8], AF.Copy, scale=0.0), "zl")
-    a.wait_ge(S.ld_u, 16)
-    a.wait_ge(S.ul, 1)
-    ar(a.activation(T.UT[:], T.U4[:, 0:4].indirect(T.UL[:, 0:32]), AF.Copy), "ut")
-
     vr(v.memset(T.ON[:], 1.0), "on")
+    fin = permute_tables(g, T, C, 0)
+    iota(T.D0[:], [[128, 4], [1, 16]], 0, "io3")
+    g.wait_ge(S.on, 1)
+    g.affine_select(T.MM[:], T.ON[:], [[-1, 516]], A.is_equal, 0.0, 3, 4).then_inc(S.mst, 1)
+    iota(T.IO[:], [[1, 512]], 0, "io4")
     v.wait_ge(S.io1, 1)
     ts(T.VJ[:], T.VI[:], 3, None, A.bitwise_and)
+    ts(T.VK[:], T.VI[:, 0:2], 112, None, A.bitwise_and)
+    at = {0: 0, 3: 260, 1: 520, 2: 1160}
+    for b in (0, 3):
+        vr(v.memset(T.CM[:, at[b] + 256:at[b] + 260], -32.0))
+    vr(v.memset(T.HB[:, 0:1], -0.5))
+    vr(v.memset(T.HB[:, 1:2], 0.5), "zy")
     vsync()
-    vr(v.tensor_copy(T.UL[:], T.VJ[:]), "ul")
-    v.wait_ge(S.io2, 1)
-    ci = lambda k: T.CI[:, 2 * k:2 * k + 2]
-    cf = lambda k: T.CF[:, 2 * k:2 * k + 2]
-    ts(ci(0), T.V2[:], 14, None, A.bitwise_and)
-    ts(ci(1), T.V2[:], 12, None, A.bitwise_and)
-    ts(ci(2), T.V2[:], 1, None, A.bitwise_and)
-    ts(ci(3), T.V2[:], 1, 1, A.arith_shift_right, A.bitwise_and)
-    ts(ci(4), T.V2[:], 4, 1, A.arith_shift_right, A.bitwise_and)
-    ts(ci(5), T.V2[:], 128, None, A.bitwise_and)
-    ts(ci(6), T.V2[:], 31, None, A.bitwise_and)
-    ts(ci(7), T.V2[:], 112, None, A.bitwise_and)
-    vsync()
-    vr(v.tensor_copy(T.CF[:, 0:16], T.CI[:, 0:16]))
-    vsync()
-    tt(cf(8), cf(3), cf(4), A.mult)
-    ts(cf(11), cf(1), 8.0, None, A.mult)
-    ts(cf(12), cf(2), 16.0, None, A.mult)
-    ts(cf(13), cf(3), 192.0, None, A.mult)
-    ts(cf(14), cf(4), 160.0, None, A.mult)
+    cp(T.UL[:], T.VJ[:], "ul")
+    cp(T.CF[:], T.VK[:])
+    fin()
     v.wait_ge(S.io3, 1)
-    ts(T.DD[:], T.D0[:], T.CF[:, 14:15], None, A.add)
-    v.wait_ge(S.io4, 1)
-    ts(T.RM[:], T.R0[:], 1.0, None, A.min)
-    vsync()
-    ts(cf(15), cf(8), 352.0, None, A.mult)
-    tt(cf(25), cf(5), cf(11), A.add)
-    tt(cf(26), cf(12), cf(13), A.add)
-    vsync()
-    tt(cf(27), cf(14), cf(15), A.subtract)
-    tt(cf(28), cf(25), cf(26), A.add)
-    vsync()
-    tt(T.SE[:, 0:2], cf(28), cf(27), A.add)
-
-    v.wait_ge(S.ut, 1)
-    vr(v.quantize_mx(T.UQ[:], T.UP[:], T.UT[:]), "uq")
-    for h in range(2):
-        v.wait_ge(S["ld_g%d" % h], 16)
-        c = slice(256 * h, 256 * h + 256)
-        vr(v.quantize_mx(T.GQ[:, c], T.GP[:, c], T.GR[:, 1024 * h:1024 * h + 1024]), "gq%d" % h)
-    v.wait_ge(S.mst, 1)
+    ts(T.DD[:], T.D0[:], T.CF[:, 0:1], None, A.add)
+    a.wait_ge(S.on, 1)
     for b in range(4):
-        vr(v.quantize_mx(T.EQ[:, 128 * b:128 * b + 128], T.EP[:, 128 * b:128 * b + 128], T.MM[:, 3 - b:515 - b]), "eq")
+        act(T.Y[:, W * b:W * b + 8], T.ON[:, 0:8], ev="u0", scale=0.0)
+
+    for q in (a, v):
+        q.wait_ge(S.ld_u, 16)
+    a.wait_ge(S.ul, 1)
+    act(T.UT[:, 256:512], T.U4[:, 0:4].indirect(T.UL[:, 16:32]), ev="ut")
+    cp(T.UT[:, 0:256], T.U4[:, 0:4].indirect(T.UL[:, 0:16]), "ut")
+    for q in range(4):
+        v.wait_ge(S["ld%d" % q], 16)
+        vr(v.quantize_mx(T.GQ[:, blk(q)], T.GP[:, blk(q)], T.GR[:, 512 * q:512 * q + 512]), "gq%d" % q)
+        if q == 0:
+            v.wait_ge(S.ut, 2)
+            vr(v.quantize_mx(T.UQ[:], T.UP[:], T.UT[:]), "uq")
     t.wait_ge(S.uq, 1)
+    for q in range(4):
+        t.wait_ge(S["gq%d" % q], 1)
+        t.matmul_mx(bank(q, 128), T.UQ[:], T.UP[:], T.GQ[:, blk(q)], T.GP[:, blk(q)], True, True).then_inc(S["ms%d" % q], 1)
+        t.matmul_mx(bank(4 + q, 128), T.GQ[:, blk(q)], T.GP[:, blk(q)], T.UQ[:], T.UP[:], True, True).then_inc(S.mc, 1)
+    for q in range(4):
+        a.wait_ge(S["ms%d" % q], 1)
+        act(T.SR[:, blk(q)], bank(q, 128), AF.Abs, "sr")
+        if q % 2:
+            a.wait_ge(S.mc, q + 1)
+            act(T.SCO[:, q - 1:q + 1], T.PS[:, 512 * (3 + q):512 * (5 + q):512], AF.Abs, "sco")
     for h in range(2):
-        t.wait_ge(S["gq%d" % h], 1)
-        c = slice(256 * h, 256 * h + 256)
-        t.matmul_mx(T.PS[:, 512 * h:512 * h + 256], T.UQ[:], T.UP[:], T.GQ[:, c], T.GP[:, c], True, True).then_inc(S["ms%d" % h], 1)
-    for b in range(4):
-        c = slice(128 * b, 128 * b + 128)
-        t.matmul_mx(T.PS[:, 2048 + 512 * b:2176 + 512 * b], T.GQ[:, c], T.GP[:, c], T.UQ[:], T.UP[:], True, True).then_inc(S.t, 1)
-    for h in range(2):
-        a.wait_ge(S["ms%d" % h], 1)
-        ar(a.activation(T.SR[:, 256 * h:256 * h + 256], T.PS[:, 512 * h:512 * h + 256], AF.Abs), "sr")
-    a.wait_ge(S.t, 4)
-    ar(a.activation(T.SCO[:], T.PS[:, 2048:4096:512], AF.Abs), "sco")
-    async_()
-    ar(a.activation(T.SN[:], T.SCO[:], AF.Copy, scale=-1.0))
-    async_()
-    for b in (2, 3):
-        ar(a.activation(T.SG[:, 512 * b - 1024:512 * b - 512], T.SR[:], AF.Sign, bias=T.SN[:, b:b + 1]), "sg")
-    for k in range(4):
-        ar(a.activation(T.ER[:, 512 * k:512 * k + 512], T.GR[:, 512 * k:512 * k + 512], AF.Copy), "er0")
+        g.wait_ge(S.sr, 2 * h + 2)
+        g.affine_select(T.SL[:, 256 * h:256 * h + 256], T.SR[:, 256 * h:256 * h + 256], [[0, 2], [-1, 128]], A.is_gt, -1.0, 0, 1).then_inc(S.sl, 1)
 
+    async_()
+    for h, (b, lo) in enumerate(((0, 128), (3, 0))):
+        act(T.SG[:, 384 * h:384 * h + 384], T.SR[:, lo:lo + 384], AF.Sign, "a" if h else "mo", bias=T.SCO[:, b:b + 1], scale=-1.0)
+    a.wait_ge(S.zy, 1)
+    for h in range(2):
+        a.wait_ge(S.mo, 1) if h == 0 else async_()
+        sg = T.SG[:, 384 * h:384 * h + 384]
+        act(sg, sg, AF.Sign, "cnt", bias=T.HB[:, h:h + 1], scale=-1.0, accum_out=T.AS[:, h:h + 1])
+    for k in range(2):
+        act(T.ER[:, 512 * k:512 * k + 512], T.GR[:, 512 * k:512 * k + 512], ev="er0")
+
+    def cmp(b, z, src, op):
+        ts(T.CM[:, at[b] + z:at[b] + z + src.stop - src.start], (T.SL if op == A.is_equal else T.SR)[:, src], T.SCO[:, b:b + 1], 2.0, op, A.mult)
+
+    def count(b, n, first):
+        z = at[b]
+        vr(v.tensor_tensor_scan(T.CN[:, 320 * b + 320 - n:320 * b + 320], T.CM[:, z:z + n], T.CM[:, z + n:z + 2 * n], first, A.add, A.add))
     v.wait_ge(S.sr, 2)
     v.wait_ge(S.sco, 1)
-
-    def before(b):
-        z = 640 * b
-        s, x = (T.SCO[:, b:b + 1], lambda i, j: T.SR[:, i:j]) if b < 2 else (0.0, lambda i, j: T.SG[:, 512 * b - 1024 + i:512 * b - 1024 + j])
-        if b:
-            ts(T.CM[:, z:z + 128 * b], x(0, 128 * b), s, None, A.is_ge)
-        ts(T.CM[:, z + 128 * b:z + 512], x(128 * b, 512), s, None, A.is_gt)
-
-    def equal(b):
-        ts(T.CM[:, 640 * b + 512:640 * b + 640], T.SL[:, 128 * b:128 * b + 128], T.SCO[:, b:b + 1], None, A.is_equal)
-
-    def count(b):
-        z = 640 * b
-        vr(v.tensor_tensor_scan(T.CN[:, 320 * b:320 * b + 320], T.CM[:, z:z + 320], T.CM[:, z + 320:z + 640], -256.0, A.add, A.add))
-    before(0)
-    before(1)
+    cmp(0, 0, blk(0), A.is_gt)
+    cmp(1, 0, blk(0), A.is_ge)
+    cmp(1, 128, blk(1), A.is_gt)
+    v.wait_ge(S.sr, 4)
+    cmp(1, 256, slice(256, 512), A.is_gt)
+    v.wait_ge(S.sco, 2)
+    cmp(2, 0, slice(0, 256), A.is_ge)
     v.wait_ge(S.sl, 1)
-    for b in range(4):
-        equal(b)
-    v.wait_ge(S.sg, 2)
-    before(2)
+    cmp(1, 512, blk(1), A.is_equal)
+    cmp(0, 128, blk(0), A.is_equal)
+    cmp(2, 256, slice(256, 512), A.is_gt)
+    cmp(3, 0, blk(3), A.is_gt)
+    v.wait_ge(S.sl, 2)
+    cmp(2, 512, blk(2), A.is_equal)
     vsync()
-    before(3)
-    for b in range(3):
-        count(b)
+    cmp(3, 128, blk(3), A.is_equal)
+    count(1, 320, -512.0)
+    count(2, 320, -512.0)
     vsync()
-    count(3)
+    for h, b in enumerate((0, 3)):
+        v.wait_ge(S.cnt, h + 1)
+        count(b, 130, T.AS[:, h:h + 1])
     vsync()
-
-    def permute(val, out, between=None):
-        vr(v.tensor_copy(T.WW[:, 0:1056].indirect(T.OFF[:, 0:8]), val))
-        vsync()
-        if between:
-            between()
-        vr(v.transpose(T.TT[:, 0:160], T.WW[:, 0:160]))
-        vr(v.transpose(T.TT[:, 160:352], T.WW[:, 512:704]))
-        vsync()
-        vr(v.tensor_copy(T.XX[:], T.TT[:, 0:448].indirect(T.SE[:, 0:2])), "xx")
-        n = vsync()["xx"]
-        a.wait_ge(S.xx, n)
-        vr(v.tensor_copy(T.ZZ[:, 0:80:4], T.XX[:, 0:20]))
-        for p in (0, 64):
-            vr(v.tensor_copy(T.ZZ[64 - p:128 - p, 2:80:4], T.XX[p:p + 64, 0:20]))
-        for d in (1, 3):
-            for p in range(4):
-                o = 32 * (p ^ d)
-                dst, src = T.ZZ[o:o + 32, d:80:4], T.XX[32 * p:32 * p + 32, 0:20]
-                if d == 1 and p < 3:
-                    vr(v.tensor_copy(dst, src))
-                else:
-                    ar(a.activation(dst, src, AF.Copy), "za")
-        vsync()
-        v.wait_ge(S.za, 5 * n)
-        vr(v.tensor_tensor_scan(out[:], T.RM[:], T.ZZ[:], 0.0, A.mult, A.add))
-        vsync()
-        return out[:, 7:80:8]
-
     rk = T.CN[:, 319:1280:320]
-    ts(T.OFF[:, 0:4], rk, 256.0, None, A.add)
-    ts(T.OFF[:, 4:8], rk, 784.0, None, A.add)
-    ts(T.QM[:], rk, -96.0, None, A.is_lt)
-    ts(T.QX[:], rk, float(264 + K * r), None, A.add)
+    ts(T.OFF[:, 0:4], rk, 0.5, 272.0, A.mult, A.add)
+    cp(T.RO[:, 0:4], rk, "rks")
     vsync()
-    v.wait_ge(S.zw, 3)
-    tt(T.QS[:], T.QM[:], T.QX[:], A.mult)
-    num = permute(T.DD[:], T.SC, lambda: ts(T.RK[:, 8 * r:8 * r + 4], T.QS[:], 0.0, None, A.add, ev="rks"))
+    num = permute(g, T, C, T.DD[:], 4)
     for k in (2, 3, 0, 1):
         ts(T.LT[:, L * k:L * k + L], num, 4.0, float(k), A.mult, A.add, ev="lt" if k > 1 else None)
 
     a.wait_ge(S.lt, 2)
     for k in (2, 3):
-        ar(a.activation(T.CG[:, k:4 * K:4], T.GR[:].indirect(T.LT[:, L * k:L * k + L]), AF.Copy), "ga")
+        act(T.CG[:, k:4 * K:4], T.GR[:].indirect(T.LT[:, L * k:L * k + L]), ev="ga")
     vsync()
     for k in (0, 1):
-        vr(v.tensor_copy(T.CG[:, k:4 * K:4], T.GR[:].indirect(T.LT[:, L * k:L * k + L])))
+        cp(T.CG[:, k:4 * K:4], T.GR[:].indirect(T.LT[:, L * k:L * k + L]))
     vsync()
     v.wait_ge(S.ga, 2)
     own = slice(K * r, K * r + K)
     vr(v.quantize_mx(T.RC[:, own], T.RP[:, own], T.CG[:]), "qc")
+    v.wait_ge(S.mst, 1)
+    for b in range(4):
+        vr(v.quantize_mx(T.EQ[:, blk(b)], T.EP[:, blk(b)], T.MM[:, 3 - b:515 - b]), "eq")
     ts(T.LP[:, 0:L], num, 0.0, None, A.add, ev="lst")
     ts(T.LP[:, L:16], T.SC[:, 7:55:8], 0.0, None, A.add, ev="lst")
 
     others, roads = plan(T, topo, r)
     off, ne = topo.mask(core, others[0]), len(topo.engines(core, others[0]))
     hs = [c for c, _ in roads[1:]]
-    on = topo.mask(core, hs[0]) & ~off if hs else 0
-    n_on = len(topo.engines(core, hs[0])) - ne if hs else 0
-    direct = roads[0][1]
+    on, n_on = topo.mask(core, hs[0]) & ~off, len(topo.engines(core, hs[0])) - ne
     sent = [0]
 
     def send(trs, n):
         g.remote_dma_fused(trs, local_sem=S.sent)
         sent[0] += n
-
-    def out(src, sem, hsem):
-        trs = []
-        if hs:
-            trs.append(transfer(topo, src, hs, on, S[hsem]))
-        if direct:
-            trs.append(transfer(topo, src, direct, off, S[sem]))
-        send(trs, (n_on if hs else 0) + (ne if direct else 0))
+    users = [s for s in range(1, N) if s >= r] + [0]
     g.wait_ge(S.rks, 1)
-    send([transfer(topo, T.RK[:, 8 * r:8 * r + 4], others, off, S["rk%d" % r])], ne)
+    send([transfer(topo, T.RO[:, 0:4], [lister(T, topo, s) for s in users], off, S.rk,
+                   [T.RO[:, 0:4] if s == r > 0 else T.RK[:, 8 * r + 8:8 * r + 12] for s in users])], ne)
     g.wait_ge(S.qc, 1)
-    out(T.RP[:, own], "ar%d" % r, "hp")
-    out(T.RC[:, own].bitcast(dt.uint8), "ar%d" % r, "hc")
-
-    mixed = lambda s: s not in (0, r)
-
-    def free(n):
-        t.wait_ge(S["vc%d" % n], 3 if mixed(order[n]) else 4)
-        if mixed(order[n]):
-            t.wait_ge(S.c3, order[n])
-
-    def decode(n):
-        s = order[n]
-        if n == 0:
-            t.wait_ge(S.qc, 1)
-            t.wait_ge(S.eq, 4)
-            t.wait_ge(S.sr, 2)
-        else:
-            t.wait_ge(S["ar%d" % s], 2 * ne)
-            if n == 1:
-                t.wait_ge(S.sco, 1)
-            else:
-                free(n - 2)
-        z = 2048 * (n % 2)
-        for b in range(4):
-            t.matmul_mx(T.PS[:, z + 512 * b:z + 512 * b + K], T.EQ[:, 128 * b:128 * b + 128], T.EP[:, 128 * b:128 * b + 128],
-                        T.RC[:, K * s:K * s + K], T.RP[:, K * s:K * s + K], True, True).then_inc(S["mm%d" % n], 1)
-
-    def unload(n):
-        s, z = order[n], 2048 * (n % 2)
-        a.wait_ge(S["mm%d" % n], 4)
-        for b in range(3 if mixed(s) else 4):
-            o = W * b + 8 + K * s
-            ar(a.activation(T.Y[:, o:o + K], T.PS[:, z + 512 * b:z + 512 * b + K], AF.Copy), "vc%d" % n)
-    for n in range(N):
-        decode(n)
-
-    a.wait_ge(S.io6, 1)
-    a.wait_ge(S.lst, 2)
-    ar(a.activation(T.NB[:], T.IO[:].indirect(T.LP[:]), AF.Copy), "nb")
-    ar(a.activation(T.SO[:], T.SR[:].indirect(T.LP[:, 0:L]), AF.Copy), "so")
-
-    ts(cf(9), cf(2), T.CF[:, 8:9], None, A.mult)
-    ts(cf(16), cf(0), 0.5, None, A.mult)
-    ts(cf(17), cf(5), 0.0625, None, A.mult)
-    tt(cf(18), cf(2), cf(4), A.add)
-    v.wait_ge(S.io5, 1)
-    ts(T.RN[:], T.R1[:], 1.0, None, A.min)
-    v.wait_ge(S.io7, 1)
-    ts(T.SD[:], T.D8[:], T.CF[:, 12:13], None, A.add)
-    vsync()
-    ts(cf(19), cf(9), 64.0, None, A.mult)
-    ts(cf(20), cf(18), 32.0, None, A.mult)
-    tt(cf(21), cf(16), cf(17), A.add)
-    vsync()
-    tt(cf(22), cf(20), cf(19), A.subtract)
-    vsync()
-    tt(T.SE[:, 2:4], cf(21), cf(22), A.add)
-
-    v.wait_ge(S.mm0, 4)
-    for b in range(4):
-        tt(T.DF[:, K * b:K * b + K], T.CG[:, b:4 * K:4], T.PS[:, 512 * b:512 * b + K], A.subtract, ev="df")
-    a.wait_ge(S.df, 4)
-    unload(0)
-
-    for s in order[1:]:
-        v.wait_ge(S["rk%d" % s], ne)
-    for b in range(4):
-        vr(v.tensor_copy(T.QV[:, N * b:N * b + N], T.RK[:, b:8 * N:8]))
-    vsync()
-    vr(v.tensor_tensor_scan(T.PX[:], T.RN[:], T.QV[:], 0.0, A.mult, A.max), "px")
-    vsync()
-    v.wait_ge(S.zl, 6)
-    pl = lambda s: T.PL[:, 16 * s:16 * s + L]
-    if r:
-        for b in range(4):
-            c = N * b + r - 1
-            ts(T.EX[:, 32 * b:32 * b + 32], T.ZT[:], T.PX[:, c:c + 1], None, A.add)
-        vsync()
-        vr(v.transpose(T.ET[:], T.EX[:]))
-        vsync()
-        vr(v.tensor_copy(T.D2[:], T.ET[:].indirect(T.SD[:, 0:8])))
-        vsync()
-        ts(pl(r), permute(T.D2[:], T.S2), 0.0, None, A.add, ev="pls")
-        g.wait_ge(S.pls, 1)
-        send([transfer(topo, pl(r), others, off, S["pl%d" % r])], ne)
+    for src, hsem in ((T.RP[:, own], S.hp), (T.RC[:, own].bitcast(dt.uint8), S.hc)):
+        g.remote_dma_fused([transfer(topo, src, hs, on, hsem), transfer(topo, src, roads[0][1], off, S["ar%d" % r])], local_sem=S.left)
     g.wait_ge(S.nd, 16)
     send([transfer(topo, T.ND[r], others, off, S["li%d" % r])], ne)
-    a.wait_ge(S.px, 1)
-    for p in range(4):
-        for d in range(4):
-            ar(a.activation(T.LQ[32 * d:32 * d + 32, p:16:4], T.PX[32 * p:32 * p + 32, N - 1:4 * N:N], AF.Copy), "lq")
 
+    def decode(out, b, cols, ev):
+        t.matmul_mx(out, T.EQ[:, blk(b)], T.EP[:, blk(b)], T.RC[:, cols], T.RP[:, cols], True, True).then_inc(S[ev], 1)
+    t.wait_ge(S.qc, 1)
+    t.wait_ge(S.sr, 4)
+    t.wait_ge(S.sco, 2)
+    for b in range(4):
+        t.wait_ge(S.eq, b + 1)
+        decode(bank(b, K), b, own, "mm3")
+    for b in range(4):
+        v.wait_ge(S.mm3, b + 1)
+        tt(T.DF[:, K * b:K * b + K], T.CG[:, b:4 * K:4], bank(b, K), A.subtract, ev="df")
+    for k in (2, 3):
+        act(T.ER[:, 512 * k:512 * k + 512], T.GR[:, 512 * k:512 * k + 512], ev="er0")
     vsync()
     v.wait_ge(S.er0, 4)
-    vr(v.tensor_copy(T.ER[:].indirect(T.LT[:, 0:40]), T.DF[:]), "erx")
-    v.wait_ge(S.lq, 16)
-    vr(v.transpose(T.LA[:], T.LQ[:, 0:32]))
-    vsync()
-    vr(v.tensor_copy(T.LB[:, 0:16], T.LA[:, 16:32]))
-    vr(v.tensor_copy(T.LB[:, 16:32], T.LA[:, 0:16]))
-    vsync()
-    vr(v.transpose(T.LQ[:, 32:64], T.LB[:]))
-    vsync()
-    vr(v.tensor_copy(T.LL[:], T.LQ[:].indirect(T.SE[:, 2:4])), "ll")
-    vsync()
+    cp(T.ER[:].indirect(T.LT[:, 0:40]), T.DF[:], "erx")
 
-    tm = lambda s: T.TM[:, K * (s % 2):K * (s % 2) + K]
-    for n in range(1, N):
-        s = order[n]
-        unload(n)
-        if mixed(s):
-            if s == 1 or (s == 2 and r == 1):
-                async_()
-            a.wait_ge(S["pl%d" % s], ne)
-            if s > 1:
-                a.wait_ge(S.c3, s - 1)
-            ar(a.activation(tm(s), T.Y[:, 3 * W:3 * W + 8 + K * s].indirect(pl(s)), AF.Copy), "tm")
-    nt = 0
+    a.wait_ge(S.io4, 1)
+    a.wait_ge(S.lst, 2)
+    act(T.NB[:], T.IO[:].indirect(T.LP[:]), ev="nb")
+    act(T.SO[:], T.SR[:].indirect(T.LP[:, 0:L]), ev="so")
+
+    where = lambda b, n: 3 * MIXED.index(b) + n if b in MIXED else 6 + PLAIN.index(b)
+    t.wait_ge(S.df, 4)
+    for n in range(3):
+        for s in (2 * n, 2 * n + 1):
+            if s != r:
+                t.wait_ge(S["ar%d" % s], 2 * ne)
+        for b in (PLAIN + MIXED if n else MIXED[:1] + PLAIN + MIXED[1:]):
+            if b in PLAIN and n:
+                t.wait_ge(S["un%d" % b], n)
+            decode(bank(where(b, n), 2 * K), b, slice(2 * K * n, 2 * K * n + 2 * K), "mm%d" % n)
+
+    def unload(n, b, k, w):
+        a.wait_ge(S["mm%d" % n], k)
+        o = W * b + 8 + 2 * K * n
+        act(T.Y[:, o:o + w], bank(where(b, n), w), ev="un%d" % b)
+    tm = lambda b, s: T.TM[:, K * (2 * MIXED.index(b) + s % 2):K * (2 * MIXED.index(b) + s % 2) + K]
+    pl = lambda s: T.PL[:, 16 * s:16 * s + L]
+
+    unload(0, MIXED[0], 1, K)
+    for k, b in enumerate(PLAIN):
+        v.wait_ge(S.mm0, 2 + k)
+        cp(T.Y[:, W * b + 8:W * b + 8 + 2 * K], bank(where(b, 0), 2 * K), "un%d" % b)
+    unload(0, MIXED[1], 4, K)
+    later = {1: [(1, PLAIN[0], 1), (1, PLAIN[1], 2)], 2: [(2, PLAIN[0], 1)], 3: [(2, PLAIN[1], 2)]}
+    a.wait_ge(S.u0, 4)
+    v.wait_ge(S.u0, 4)
     for s in range(1, N):
-        if s != r:
-            v.wait_ge(S["pl%d" % s], ne)
-        for k in ([0, 1] if s == 1 else [s]):
-            v.wait_ge(S["vc%d" % turn[k]], 3 if mixed(k) else 4)
-        for b in (3, 0, 1, 2):
+        a.wait_ge(S["pl%d" % s], ne)
+        for b in MIXED:
+            a.wait_ge(S["c%d" % b], s - 1) if s > 1 else a.wait_ge(S["un%d" % b], 1)
+            act(tm(b, s), T.Y[:, W * b:W * b + 8 + K * s].indirect(pl(s)), ev="tm%d" % b)
+        for n, b, k in later.get(s, ()):
+            unload(n, b, k, 2 * K)
+        v.wait_ge(S["pl%d" % s], ne)
+        for b in PLAIN + MIXED:
             o = W * b + 8 + K * s
-            if s > 1:
-                v.wait_ge(S["c%d" % b], s - 1)
-            if b == 3 and mixed(s):
-                nt += 1
-                v.wait_ge(S.tm, nt)
-                z = 2048 * (turn[s] % 2) + 512 * b
-                tt(T.Y[:, o:o + K], tm(s), T.PS[:, z:z + K], A.add, ev="c3")
-            else:
+            if b in PLAIN:
+                v.wait_ge(S["un%d" % b], s // 2 + 1)
+                if s > 1:
+                    v.wait_ge(S["c%d" % b], s - 1)
                 tt(T.Y[:, o:o + K], T.Y[:, W * b:o].indirect(pl(s)), T.Y[:, o:o + K], A.add, ev="c%d" % b)
+            else:
+                v.wait_ge(S["mm%d" % (s // 2)], 4)
+                v.wait_ge(S["tm%d" % b], s)
+                z = 512 * where(b, s // 2) + K * (s % 2)
+                tt(T.Y[:, o:o + K], tm(b, s), T.PS[:, z:z + K], A.add, ev="c%d" % b)
 
-    def lay(b, h):
-        return T.AC[:, 512 * h + b:512 * h + 512:4], T.Y[:, W * b:W * b + W].indirect(T.LL[:, 8 * h:8 * h + 8])
-
-    def lay_a(b, h):
-        dst, win = lay(b, h)
-        ar(a.activation(dst, win, AF.Copy), "fa%d" % h)
-    a.wait_ge(S.ll, 1)
-    a.wait_ge(S.c3, N - 1)
+    for q in (a, v):
+        q.wait_ge(S.ll, ne)
     for h in range(4):
-        lay_a(3, h)
-    a.wait_ge(S.c2, N - 1)
-    a.wait_ge(S.c1, N - 1)
-    v.wait_ge(S.c0, N - 1)
-    for h in range(4):
-        for b in ((0, 1) if h < 2 else (0,)):
-            if h == 0 and b == 1:
-                v.wait_ge(S.c1, N - 1)
-            dst, win = lay(b, h)
-            vr(v.tensor_copy(dst, win), "fv%d" % h)
-        for b in ((2,) if h < 2 else (2, 1)):
-            lay_a(b, h)
+        for b in range(4):
+            dst, win = T.AC[:, 512 * h + b:512 * h + 512:4], T.Y[:, W * b:W * b + W].indirect(T.LL[:, 8 * h:8 * h + 8])
+            if h == 0:
+                (a if b in PLAIN else v).wait_ge(S["c%d" % b], N - 1)
+            if b in PLAIN:
+                act(dst, win, ev="fa%d" % h)
+            else:
+                cp(dst, win, "fv%d" % h)
     vsync()
+    async_()
 
     sy.wait_ge(S.nb, 1)
     sy.dma_start(T.ND[r], T.NB[0:1, :]).then_inc(S.nd, 16)
@@ -480,13 +487,15 @@ def rank_program(g, core, T, topo):
     sy.wait_ge(S.so, 1)
     sy.dma_start(T.sc[:], T.SO[0:1, :]).then_inc(S.st, 16)
     sy.wait_ge(S.erx, 1)
+    sy.wait_ge(S.left, 2 * (n_on + ne))
     sy.dma_start(T.er[:], T.ER[:]).then_inc(S.st, 16)
-    for s in order[1:]:
-        sy.wait_ge(S["li%d" % s], ne)
-        sy.dma_start(T.nb[s:s + 1, :], T.ND[s, 0:K // 2, :]).then_inc(S.st, 16)
+    for s in range(N):
+        if s != r:
+            sy.wait_ge(S["li%d" % s], ne)
+            sy.dma_start(T.nb[s:s + 1, :], T.ND[s, 0:K // 2, :]).then_inc(S.st, 16)
     for h in range(4):
-        sy.wait_ge(S["fv%d" % h], 2 if h < 2 else 1)
-        sy.wait_ge(S["fa%d" % h], 2 if h < 2 else 3)
+        sy.wait_ge(S["fv%d" % h], 2)
+        sy.wait_ge(S["fa%d" % h], 2)
         sy.dma_start(T.acc[:, 512 * h:512 * h + 512], T.AC[:, 512 * h:512 * h + 512]).then_inc(S.st, 16)
     g.wait_ge(S.sent, sent[0])
     sy.wait_ge(S.st, 16 * (N + 6))

@@ -4,7 +4,20 @@ from concourse.mybir import dt, AluOpType, ActivationFunctionType
 N, TC, K = 6, 512, 160
 W = 8 + N * K
 L = K // 16
-SHARE = [(3, 1, 1)] * N
+CORES_ALL = 128
+HOST = [(1, 1, 1, (1, 2, 3)), (1, 0, 1, (0, 4, 5)), (2, 1, 2, (1, 4, 5)), (2, 0, 2, (0, 2, 3)), (3, 3, 1, range(N)), (4, 4, 1, range(N)), (5, 5, 1, (5, 0, 1)), (5, 4, 2, (4, 2, 3)), (0, 5, 2, range(N))]
+HANDS = [3, 3, 3, 3, 3, 3]
+EARLY = ()
+LATE = (5, 0)
+DELAY = 0
+DELAY2 = 0
+RING = True
+SHARE = [(2, 1, 1, 1)] * N
+ORDER = (0, 1, 2)
+EARLY_E = 1
+WIDE = True
+SPLIT = False
+GROUPS = [(0,), (1,), (2, 3), (4, 5)]
 MIXED = (3, 2)
 PLAIN = (0, 1)
 
@@ -19,26 +32,28 @@ SCRATCH = {
     "SR": ("sbuf", [128, 512], F), "SL": ("sbuf", [128, 512], F), "SCO": ("sbuf", [128, 4], F), "AS": ("sbuf", [128, 2], F),
     "HB": ("sbuf", [128, 2], F), "SG": ("sbuf", [128, 768], B), "CM": ("sbuf", [128, 1800], B), "CN": ("sbuf", [128, 1280], B),
     "OFF": ("sbuf", [128, 8], U), "DD": ("sbuf", [128, 64], F), "WW": ("sbuf", [128, 1072], F),
+    "EB": ("sbuf", [128, 128], B), "EU": ("sbuf", [128, 128], B), "WB": ("sbuf", [128, 1072], B), "TH": ("sbuf", [128, 448], B),
     "TT": ("sbuf", [128, 448], F), "XX": ("sbuf", [128, 32], F), "ZZ": ("sbuf", [128, 80], F),
     "RM": ("sbuf", [128, 80], F), "SC": ("sbuf", [128, 80], F),
     "LT": ("sbuf", [128, 40], U), "LP": ("sbuf", [128, 16], U),
-    "RO": ("sbuf", [128, 8], B), "RK": ("sbuf", [128, 64], B), "RL": ("sbuf", [128, 4], U), "BA": ("sbuf", [128, 64], F),
+    "RO": ("sbuf", [128, 8], B), "RX": ("sbuf", [128, 8], B), "RK": ("sbuf", [128, 64], B), "RL": ("sbuf", [128, 4], U), "BA": ("sbuf", [128, 64], F),
     "Q0": ("sbuf", [128, 64], F), "Q1": ("sbuf", [128, 64], F), "OP": ("sbuf", [128, 4], F),
     "EX": ("sbuf", [128, 128], F), "ET": ("sbuf", [128, 128], F),
     "LQ": ("sbuf", [128, 64], F), "LA": ("sbuf", [128, 64], F), "LF": ("sbuf", [128, 32], F),
     "CG": ("sbuf", [128, 4 * K], B), "RC": ("sbuf", [128, N * K], C8), "RP": ("sbuf", [128, N * K], P8),
     "DF": ("sbuf", [128, 4 * K], F), "ER": ("sbuf", [128, 2048], F), "Y": ("sbuf", [128, 4 * W], F), "TM": ("sbuf", [128, 4 * K], F),
     "PL": ("sbuf", [128, 16 * N], U), "LL": ("sbuf", [128, 32], U), "AC": ("sbuf", [128, 2048], F), "IO": ("sbuf", [128, 512], F),
-    "NB": ("sbuf", [128, 256], F), "ND": ("dram", [N, 128, 2], F), "SO": ("sbuf", [128, K], F),
+    "NB": ("sbuf", [128, 256], B), "ND": ("dram", [N, 128, 2], B), "NC": ("sbuf", [128, K], F), "SO": ("sbuf", [128, K], F),
     "VI": ("sbuf", [128, 32], I), "VJ": ("sbuf", [128, 32], I), "VK": ("sbuf", [128, 2], I), "UL": ("sbuf", [128, 32], U),
     "CF": ("sbuf", [128, 2], F), "SE": ("sbuf", [128, 2], U), "D0": ("sbuf", [128, 64], F),
+    "DL": ("sbuf", [128, 1024], F),
     "TA": ("sbuf", [128, 32], F), "TB": ("sbuf", [128, 32], F),
 }
 _EV = ["v", "a", "mc", "ld_u", "on", "ul", "io1", "io2", "io3", "io4", "mst", "ut", "uq", "sco", "cnt", "sl", "er0", "xx", "za", "lt",
        "eq", "rks", "px", "lq", "ga", "lst", "qc", "df", "erx", "so", "nb", "nd", "ll", "st", "sent", "hp", "hc", "hl", "rk", "mo",
-       "zy", "sr", "u0", "left"]
-SEMAPHORES = _EV + ["%s%d" % (e, n) for e in ("li", "ar", "pl") for n in range(N)] \
-    + ["%s%d" % (e, n) for e in ("ld", "gq", "ms", "fv", "fa", "c", "tm", "mm", "un") for n in range(4)]
+       "zy", "sr", "u0", "left", "mine", "rf", "dl", "li", "rkd", "nc", "n0", "n1"]
+SEMAPHORES = _EV + ["%s%d" % (e, n) for e in ("ar", "pl") for n in range(N)] \
+    + ["%s%d" % (e, n) for e in ("ld", "gq", "ms", "fv", "fa", "c", "tm", "mm", "un", "uv") for n in range(4)]
 
 A, AF = AluOpType, ActivationFunctionType
 
@@ -89,15 +104,80 @@ def plan(T, topo, r):
     others = [T.cores[(r - d) % N] for d in range(1, N)]
     hs = [c for c in topo.cores_of(core) if c != core and all(topo.may_write(c, d) for d in others)]
     hs.sort(key=lambda c: topo.die(c) == topo.die(core))
-    out, i = [], 0
-    for c, n in zip([core] + hs, SHARE[r]):
-        out.append((c, others[i:i + n]))
-        i += n
-    return others, out
+    if RING:
+        ends = [sum(SHARE[r][:n]) for n in range(len(SHARE[r]) + 1)]
+        cs = [core] + [hs[n] for n in ORDER]
+        return others, [(c, others[x:y]) for c, x, y in zip(cs, ends, ends[1:])]
+    direct, handed, _ = routes(T, topo)
+    return others, [(core, direct[r])] + [(c, [d]) for c, d in zip(hs, handed[r])]
 
 
-def lister(T, topo, s):
-    return plan(T, topo, s)[1][-1][0]
+_ROUTES = []
+
+
+def choices(options):
+    if not options:
+        return [[]]
+    return [[x] + rest for rest in choices(options[1:]) for x in options[0]]
+
+
+def routes(T, topo):
+    if _ROUTES:
+        return _ROUTES[0]
+    cores = list(T.cores)
+    chip = [topo.chip(c) for c in cores]
+    side = {s: cores[d] for s in range(N) for d in range(N) if topo.mates(chip[s], chip[d])}
+    taken = {s: [d for d in range(N) if d == s or topo.mates(chip[s], chip[d])] for s in range(N)}
+    far, first = {}, {s: [] for s in range(N)}
+    for d in range(N):
+        if d not in side:
+            idle = [c for c in range(CORES_ALL) if topo.mates(topo.chip(c), chip[d]) and topo.may_write(c, cores[d]) and topo.die(c) == topo.die(cores[d])][0]
+            s = max(x for x in range(N) if topo.same_plane(chip[x], topo.chip(idle)))
+            far[idle] = (s, cores[d])
+            first[s].append(idle)
+            taken[s].append(d)
+    rest = [[d for d in range(N) if d not in taken[s]] for s in range(N)]
+    pairs = [[(x, y) for x in rest[s] for y in rest[s] if x < y and topo.same_plane(chip[s], chip[x]) != topo.same_plane(chip[s], chip[y])]
+             for s in range(N)]
+    best = None
+    for pick in choices(pairs):
+        late = [[s for s in range(N) if d in pick[s]] for d in range(N)]
+        if all(len(x) == 2 for x in late):
+            soon = [[s for s in range(N) if d in rest[s] and d not in pick[s]] for d in range(N)]
+            worth = sorted(max(x) for x in soon + late)
+            if best is None or worth > best[0]:
+                best = (worth, pick, soon, late)
+    _, pick, soon, late = best
+    direct = [[cores[d] for d in range(N) if min(soon[d]) == s] + first[s] + ([side[s]] if s in side else [])
+              + [cores[d] for d in range(N) if max(soon[d]) == s] for s in range(N)]
+    handed = [[cores[d] for d in sorted(pick[s], key=lambda d: max(late[d]) == s)] for s in range(N)]
+    _ROUTES.append((direct, handed, far))
+    return _ROUTES[0]
+
+
+def listers(T, topo):
+    return {plan(T, topo, r)[1][n][0]: (s, to) for s, r, n, to in HOST}
+
+
+def list_of(T, topo, c):
+    return listers(T, topo).get(c, (None,))[0]
+
+
+def rank_roads(T, topo, r):
+    hs = [c for c, _ in plan(T, topo, r)[1][1:]]
+    users = {c: s for c, (s, _) in listers(T, topo).items() if s == 0 or s >= r}
+    late = [c for c, s in users.items() if c not in hs and s in LATE]
+    jobs = {c: late[n::HANDS[r]] if n < HANDS[r] else [] for n, c in enumerate(hs)}
+    return [c for c, s in users.items() if c not in hs and s not in LATE], {c: x for c, x in jobs.items() if x or c in users}
+
+
+def slot(T, r, s):
+    return T.RO[:, 0:4] if s == r > 0 else T.RK[:, 8 * r + 8:8 * r + 12]
+
+
+def landing(T, topo, r, c):
+    s = list_of(T, topo, c)
+    return slot(T, r, s) if s is not None and (s == 0 or s >= r) else T.RX[:, 0:4]
 
 
 def transfer(topo, src, cores, mask, sem, dsts=None):
@@ -119,27 +199,27 @@ def table(g, T, C, even, odd, step):
     return finish
 
 
-def permute_tables(g, T, C, col):
+def permute_tables(g, T, C, col, ww, turned):
     vr = C[0]
     fin = table(g, T, C, ([[32, 4], [192, 2], [16, 2]], col), ([[32, 4], [-160, 2], [16, 2]], 160 + col), 128)
     v = g.vector
-    vr(v.memset(T.WW[:, 0:192], 0.0))
-    vr(v.memset(T.TT[:, 352:448], 0.0))
+    vr(v.memset(ww[:, 0:192], 0.0))
+    vr(v.memset(turned[:, 352:448], 0.0))
     vr(v.memset(T.RM[:], 1.0))
     C[1]()
     vr(v.memset(T.RM[:, 0:80:8], 0.0))
     return fin
 
 
-def permute(g, T, C, val, n):
+def permute(g, T, C, val, n, ww, turned):
     vr, vsync, async_, ts, tt, cp, act, iota = C
     v, a = g.vector, g.scalar
-    cp(T.WW[:].indirect(T.OFF[:, 0:n]), val)
+    cp(ww[:].indirect(T.OFF[:, 0:n]), val)
     vsync()
-    vr(v.transpose(T.TT[:, 0:160], T.WW[:, 16:176]))
-    vr(v.transpose(T.TT[:, 160:352], T.WW[:, 0:192]))
+    vr(v.transpose(turned[:, 0:160], ww[:, 16:176]))
+    vr(v.transpose(turned[:, 160:352], ww[:, 0:192]))
     vsync()
-    cp(T.XX[:], T.TT[:].indirect(T.SE[:]), "xx")
+    cp(T.XX[:], turned[:].indirect(T.SE[:]), "xx")
     vsync()
     a.wait_ge(T.sem.xx, 1)
     cp(T.ZZ[:, 0:80:4], T.XX[:, 0:20])
@@ -160,46 +240,60 @@ def permute(g, T, C, val, n):
     return T.SC[:, 7:80:8]
 
 
-def make_list(g, T, s, ne):
+def make_list(g, T, s, ne, near):
     C = calls(g, T)
     vr, vsync, async_, ts, tt, cp, act, iota = C
     v, a, S = g.vector, g.scalar, T.sem
     m = s or N
     g.iota(T.VI[:, 0:4], [[1, 4]], 0, 8).then_inc(S.io1, 1)
-    iota(T.BA[:], [[0, 8], [2 * K, 8]], 2 * 8 + TC - 2 * K, "io3")
+    short = 0 < s and 8 + K * s <= TC
+    mid = 8 + K * s if short else 0
+    ex, et, ww, turned = (T.EB, T.EU, T.WB, T.TH) if short else (T.EX, T.ET, T.WW, T.TT)
+    iota(T.BA[:], [[0, 8], [2 * K, 8]], 2 * 8 + TC - 2 * K - mid, "io3")
+    vr(v.memset(T.HB[:, 0:1], 4096.0 * (2 * K - TC - 1)), "ul")
     if s:
-        fin = permute_tables(g, T, C, 14)
+        fin = permute_tables(g, T, C, 14, ww, turned)
     else:
         fin = table(g, T, C, ([[1, 8], [32, 2]], 0), ([[1, 8], [-32, 2]], 32), 8)
         vr(v.memset(T.LQ[:, 16:32], 0.0))
     vr(v.memset(T.RK[:, 0:8], float(2 * K - 2 * 8 - TC)))
     vr(v.memset(T.RK[:, 8 * m + 8:64], 0.0))
-    vr(v.memset(T.EX[:], 0.0))
+    vr(v.memset(ex[:], 0.0))
     v.wait_ge(S.io1, 1)
     ts(T.VJ[:, 0:4], T.VI[:, 0:4], 63, None, A.bitwise_and)
     ts(T.VK[:, 0:1], T.VI[:, 0:1], 128, None, A.bitwise_and)
     vsync()
-    cp(T.RL[:], T.VJ[:, 0:4])
+    cp(T.RL[:], T.VJ[:, 0:4], "ul")
     cp(T.CF[:, 0:1], T.VK[:, 0:1])
     fin()
     ts(T.OP[:, 0:1], T.CF[:, 0:1], 528 / 128, 272.0, A.mult, A.add)
     ts(T.OP[:, 1:2], T.CF[:, 0:1], -528 / 128, 800.0, A.mult, A.add)
     vsync()
     v.wait_ge(S.io3, 1)
-    v.wait_ge(S.rk, ne * (m + 1 if s else m))
+    arrive = ne * ((m + 1 if s else m) - bool(near))
+    v.wait_ge(S.rk, arrive)
+    if near:
+        v.wait_ge(S.rf, near)
+    if DELAY and s in LATE:
+        vr(v.memset(T.ER[:, 0:DELAY], 0.0))
     win = T.RK[:].indirect(T.RL[:])
+    a.wait_ge(S.ul, 2)
+    a.wait_ge(S.rk, arrive)
+    if near:
+        a.wait_ge(S.rf, near)
+    act(T.Q0[:], win, AF.Relu, "mo", bias=T.HB[:, 0:1], scale=-4096.0)
     tt(T.Q1[:], win, T.BA[:], A.add)
-    ts(T.Q0[:], win, float(2 * K - TC), 4096.0, A.is_lt, A.mult)
+    for h in range(2 if s else 0):
+        ts(T.OFF[:, h:8:2], T.RO[:, 0:4], 0.5, T.OP[:, h:h + 1], A.mult, A.add)
     vsync()
-    vr(v.tensor_tensor_scan(T.EX[:, 0:128:2], T.Q0[:], T.Q1[:], 0.0, A.add, A.min), "px")
+    v.wait_ge(S.mo, 1)
+    vr(v.tensor_tensor_scan(ex[:, 0:128:2], T.Q0[:], T.Q1[:], 0.0, A.add, A.min), "px")
     if s:
-        for h in range(2):
-            ts(T.OFF[:, h:8:2], T.RO[:, 0:4], 0.5, T.OP[:, h:h + 1], A.mult, A.add)
         vsync()
-        vr(v.transpose(T.ET[:], T.EX[:]))
+        vr(v.transpose(et[:], ex[:]))
         vsync()
         out = T.PL[:, 16 * s:16 * s + L]
-        ts(out, permute(g, T, C, T.ET[:], 8), 0.5, None, A.mult, ev="hl")
+        ts(out, permute(g, T, C, et[:], 8, ww, turned), 0.5, mid / 2, A.mult, A.add, ev="hl")
         vsync()
         return out, "pl%d" % s
     vsync()
@@ -227,6 +321,13 @@ def make_list(g, T, s, ne):
 
 def helper_program(g, core, T, topo):
     S = T.sem
+    if not RING and core in routes(T, topo)[2]:
+        r, to = routes(T, topo)[2][core]
+        ne = len(topo.engines(core, to))
+        g.wait_ge(S["ar%d" % r], 2 * len(topo.engines(T.cores[r], core)))
+        for src in (T.RP[:, K * r:K * r + K], T.RC[:, K * r:K * r + K].bitcast(dt.uint8)):
+            g.remote_dma_fused([transfer(topo, src, [to], topo.mask(core, to), S["ar%d" % r])], local_sem=S.sent)
+        g.wait_ge(S.sent, 2 * ne)
     for r in range(N):
         if topo.chip(T.cores[r]) != topo.chip(core):
             continue
@@ -234,17 +335,28 @@ def helper_program(g, core, T, topo):
         mask, ne = topo.mask(core, others[0]), len(topo.engines(core, others[0]))
         nin = len(topo.engines(T.cores[r], core)) - ne
         own = slice(K * r, K * r + K)
-        mine = make_list(g, T, r, ne) if core == lister(T, topo, r) else None
-        for c, dests in roads:
-            if c != core:
-                continue
-            for sem, src in (("hp", T.RP[:, own]), ("hc", T.RC[:, own].bitcast(dt.uint8))):
-                g.wait_ge(S[sem], nin)
-                g.remote_dma_fused([transfer(topo, src, dests, mask, S["ar%d" % r])], local_sem=S.sent)
-            if mine:
-                g.wait_ge(S.hl, 1)
-                g.remote_dma_fused([transfer(topo, mine[0], others + [T.cores[r]], mask, S[mine[1]])], local_sem=S.sent)
-            g.wait_ge(S.sent, (3 if mine else 2) * ne)
+        dests = dict(roads[1:]).get(core)
+        if dests is None:
+            continue
+        jobs = [("hc", nin + ne * WIDE, T.RC[:, own].bitcast(dt.uint8), dests, "ar%d" % r, None), ("hp", nin, T.RP[:, own], dests, "ar%d" % r, None)] if dests else []
+        s = list_of(T, topo, core)
+        here = LATE and s is not None and (s == 0 or s >= r)
+        if s is not None:
+            src, sem = make_list(g, T, s, ne, nin if here else 0)
+            jobs.insert(0 if s in EARLY else 2, ("hl", 1, src, [T.cores[d] for d in listers(T, topo)[core][1]], sem, None))
+        if core in rank_roads(T, topo, r)[1]:
+            late = rank_roads(T, topo, r)[1][core]
+            jobs.insert(0, ("rf", nin, landing(T, topo, r, core), late, "rk", [slot(T, r, list_of(T, topo, x)) for x in late]))
+        for wait, n, src, to, sem, dsts in jobs:
+            g.wait_ge(S[wait], n)
+            if SPLIT and wait == "hc":
+                g.remote_dma_fused([transfer(topo, T.RC[:, K * r + 80 * h:K * r + 80 * h + 80].bitcast(dt.uint8), to, mask & m, S[sem]) for h, m in enumerate((0x0F0F, 0xF0F0))], local_sem=S.sent)
+            elif wait == "hl":
+                g.remote_dma_fused([transfer(topo, src, [c for c in to if c in others], mask, S[sem]),
+                                    transfer(topo, src, [T.cores[r]], topo.mask(core, T.cores[r]) & ~mask, S[sem])], local_sem=S.sent)
+            elif to:
+                g.remote_dma_fused([transfer(topo, src, to, mask, S[sem], dsts)], local_sem=S.sent)
+        g.wait_ge(S.sent, sum(ne + nin * (job[0] == "hl") for job in jobs if job[3]))
 
 
 def rank_program(g, core, T, topo):
@@ -264,11 +376,11 @@ def rank_program(g, core, T, topo):
 
     g.iota(T.VI[:], [[0, 32]], 0, 1).then_inc(S.io1, 1)
     vr(v.memset(T.ON[:], 1.0), "on")
-    fin = permute_tables(g, T, C, 0)
-    iota(T.D0[:], [[128, 4], [1, 16]], 0, "io3")
+    fin = permute_tables(g, T, C, 0, T.WB, T.TH)
+    iota(T.D0[:], [[128, 4], [1, 16]], -256, "io3")
     g.wait_ge(S.on, 1)
     g.affine_select(T.MM[:], T.ON[:], [[-1, 516]], A.is_equal, 0.0, 3, 4).then_inc(S.mst, 1)
-    iota(T.IO[:], [[1, 512]], 0, "io4")
+    g.dma_start(T.ER[:], T.gr[:]).then_inc(S.er0, 16)
     v.wait_ge(S.io1, 1)
     ts(T.VJ[:], T.VI[:], 3, None, A.bitwise_and)
     ts(T.VK[:], T.VI[:, 0:2], 112, None, A.bitwise_and)
@@ -287,6 +399,10 @@ def rank_program(g, core, T, topo):
     for b in range(4):
         act(T.Y[:, W * b:W * b + 8], T.ON[:, 0:8], ev="u0", scale=0.0)
 
+    def ones(b):
+        v.wait_ge(S.mst, 1)
+        vr(v.quantize_mx(T.EQ[:, blk(b)], T.EP[:, blk(b)], T.MM[:, 3 - b:515 - b]), "eq")
+
     for q in (a, v):
         q.wait_ge(S.ld_u, 16)
     a.wait_ge(S.ul, 1)
@@ -298,6 +414,8 @@ def rank_program(g, core, T, topo):
         if q == 0:
             v.wait_ge(S.ut, 2)
             vr(v.quantize_mx(T.UQ[:], T.UP[:], T.UT[:]), "uq")
+        elif q - 1 < EARLY_E:
+            ones(q - 1)
     t.wait_ge(S.uq, 1)
     for q in range(4):
         t.wait_ge(S["gq%d" % q], 1)
@@ -313,6 +431,8 @@ def rank_program(g, core, T, topo):
         g.wait_ge(S.sr, 2 * h + 2)
         g.affine_select(T.SL[:, 256 * h:256 * h + 256], T.SR[:, 256 * h:256 * h + 256], [[0, 2], [-1, 128]], A.is_gt, -1.0, 0, 1).then_inc(S.sl, 1)
 
+    iota(T.NC[0:32, :], [[0, K]], 256, "nc")
+
     async_()
     for h, (b, lo) in enumerate(((0, 128), (3, 0))):
         act(T.SG[:, 384 * h:384 * h + 384], T.SR[:, lo:lo + 384], AF.Sign, "a" if h else "mo", bias=T.SCO[:, b:b + 1], scale=-1.0)
@@ -321,15 +441,13 @@ def rank_program(g, core, T, topo):
         a.wait_ge(S.mo, 1) if h == 0 else async_()
         sg = T.SG[:, 384 * h:384 * h + 384]
         act(sg, sg, AF.Sign, "cnt", bias=T.HB[:, h:h + 1], scale=-1.0, accum_out=T.AS[:, h:h + 1])
-    for k in range(2):
-        act(T.ER[:, 512 * k:512 * k + 512], T.GR[:, 512 * k:512 * k + 512], ev="er0")
 
     def cmp(b, z, src, op):
         ts(T.CM[:, at[b] + z:at[b] + z + src.stop - src.start], (T.SL if op == A.is_equal else T.SR)[:, src], T.SCO[:, b:b + 1], 2.0, op, A.mult)
 
     def count(b, n, first):
         z = at[b]
-        vr(v.tensor_tensor_scan(T.CN[:, 320 * b + 320 - n:320 * b + 320], T.CM[:, z:z + n], T.CM[:, z + n:z + 2 * n], first, A.add, A.add))
+        vr(v.tensor_tensor_scan(T.CN[:, 320 * b + 320 - n:320 * b + 320], T.CM[:, z:z + n], T.CM[:, z + n:z + 2 * n], first, A.add, A.add), "rkd")
     v.wait_ge(S.sr, 2)
     v.wait_ge(S.sco, 1)
     cmp(0, 0, blk(0), A.is_gt)
@@ -357,46 +475,56 @@ def rank_program(g, core, T, topo):
     vsync()
     rk = T.CN[:, 319:1280:320]
     ts(T.OFF[:, 0:4], rk, 0.5, 272.0, A.mult, A.add)
-    cp(T.RO[:, 0:4], rk, "rks")
     vsync()
-    num = permute(g, T, C, T.DD[:], 4)
+    a.wait_ge(S.rkd, 4)
+    act(T.RO[:, 0:4], rk, ev="rks")
+    num = permute(g, T, C, T.DD[:], 4, T.WB, T.TH)
     for k in (2, 3, 0, 1):
-        ts(T.LT[:, L * k:L * k + L], num, 4.0, float(k), A.mult, A.add, ev="lt" if k > 1 else None)
+        ts(T.LT[:, L * k:L * k + L], num, 4.0, float(1024 + k), A.mult, A.add, ev="lt")
 
-    a.wait_ge(S.lt, 2)
     for k in (2, 3):
+        a.wait_ge(S.lt, k - 1)
         act(T.CG[:, k:4 * K:4], T.GR[:].indirect(T.LT[:, L * k:L * k + L]), ev="ga")
-    vsync()
     for k in (0, 1):
+        v.wait_ge(S.lt, k + 3)
         cp(T.CG[:, k:4 * K:4], T.GR[:].indirect(T.LT[:, L * k:L * k + L]))
     vsync()
     v.wait_ge(S.ga, 2)
     own = slice(K * r, K * r + K)
     vr(v.quantize_mx(T.RC[:, own], T.RP[:, own], T.CG[:]), "qc")
-    v.wait_ge(S.mst, 1)
-    for b in range(4):
-        vr(v.quantize_mx(T.EQ[:, blk(b)], T.EP[:, blk(b)], T.MM[:, 3 - b:515 - b]), "eq")
-    ts(T.LP[:, 0:L], num, 0.0, None, A.add, ev="lst")
-    ts(T.LP[:, L:16], T.SC[:, 7:55:8], 0.0, None, A.add, ev="lst")
+    for b in range(EARLY_E, 4):
+        ones(b)
+    ts(T.LP[:, 0:L], num, 256.0, None, A.add, ev="lst")
+    ts(T.LP[:, L:16], T.SC[:, 7:55:8], 256.0, None, A.add, ev="lst")
 
     others, roads = plan(T, topo, r)
     off, ne = topo.mask(core, others[0]), len(topo.engines(core, others[0]))
-    hs = [c for c, _ in roads[1:]]
-    on, n_on = topo.mask(core, hs[0]) & ~off, len(topo.engines(core, hs[0])) - ne
+    hs = [c for c, d in roads[1:] if d]
+    on, n_on = topo.mask(core, roads[1][0]) & ~off, len(topo.engines(core, roads[1][0])) - ne
     sent = [0]
 
     def send(trs, n):
         g.remote_dma_fused(trs, local_sem=S.sent)
         sent[0] += n
-    users = [s for s in range(1, N) if s >= r] + [0]
+    early, late = rank_roads(T, topo, r)
+    trs = [transfer(topo, T.RO[:, 0:4], list(late), on, S.rf, [landing(T, topo, r, c) for c in late])] if late else []
+    if early:
+        trs.append(transfer(topo, T.RO[:, 0:4], early, off, S.rk, [slot(T, r, list_of(T, topo, c)) for c in early]))
     g.wait_ge(S.rks, 1)
-    send([transfer(topo, T.RO[:, 0:4], [lister(T, topo, s) for s in users], off, S.rk,
-                   [T.RO[:, 0:4] if s == r > 0 else T.RK[:, 8 * r + 8:8 * r + 12] for s in users])], ne)
+    send(trs, n_on * bool(late) + ne * bool(early))
     g.wait_ge(S.qc, 1)
-    for src, hsem in ((T.RP[:, own], S.hp), (T.RC[:, own].bitcast(dt.uint8), S.hc)):
-        g.remote_dma_fused([transfer(topo, src, hs, on, hsem), transfer(topo, src, roads[0][1], off, S["ar%d" % r])], local_sem=S.left)
+    if DELAY2:
+        iota(T.DL[:, 0:DELAY2], [[1, DELAY2]], 0, "dl")
+        g.wait_ge(S.dl, 1)
+    planes, codes, direct = T.RP[:, own], T.RC[:, own].bitcast(dt.uint8), (roads[0][1], off, S["ar%d" % r])
+    for call in ([(codes, hs, on | off * WIDE, S.hc)], [(planes, hs, on, S.hp), (planes,) + direct], [(codes,) + direct]):
+        if any(w[1] for w in call):
+            if SPLIT and call[0][0] is codes:
+                call = [(T.RC[:, K * r + 80 * h:K * r + 80 * h + 80].bitcast(dt.uint8), call[0][1], call[0][2] & m, call[0][3]) for h, m in enumerate((0x0F0F, 0xF0F0))]
+            g.remote_dma_fused([transfer(topo, *w) for w in call if w[1]], local_sem=S.left)
+    iota(T.IO[:], [[1, 512]], -256, "io4")
     g.wait_ge(S.nd, 16)
-    send([transfer(topo, T.ND[r], others, off, S["li%d" % r])], ne)
+    send([transfer(topo, T.ND[r], others, off, S.li)], ne)
 
     def decode(out, b, cols, ev):
         t.matmul_mx(out, T.EQ[:, blk(b)], T.EP[:, blk(b)], T.RC[:, cols], T.RP[:, cols], True, True).then_inc(S[ev], 1)
@@ -405,14 +533,12 @@ def rank_program(g, core, T, topo):
     t.wait_ge(S.sco, 2)
     for b in range(4):
         t.wait_ge(S.eq, b + 1)
-        decode(bank(b, K), b, own, "mm3")
+        decode(bank(b, K), b, own, "mine")
     for b in range(4):
-        v.wait_ge(S.mm3, b + 1)
+        v.wait_ge(S.mine, b + 1)
         tt(T.DF[:, K * b:K * b + K], T.CG[:, b:4 * K:4], bank(b, K), A.subtract, ev="df")
-    for k in (2, 3):
-        act(T.ER[:, 512 * k:512 * k + 512], T.GR[:, 512 * k:512 * k + 512], ev="er0")
     vsync()
-    v.wait_ge(S.er0, 4)
+    v.wait_ge(S.er0, 16)
     cp(T.ER[:].indirect(T.LT[:, 0:40]), T.DF[:], "erx")
 
     a.wait_ge(S.io4, 1)
@@ -420,30 +546,38 @@ def rank_program(g, core, T, topo):
     act(T.NB[:], T.IO[:].indirect(T.LP[:]), ev="nb")
     act(T.SO[:], T.SR[:].indirect(T.LP[:, 0:L]), ev="so")
 
-    where = lambda b, n: 3 * MIXED.index(b) + n if b in MIXED else 6 + PLAIN.index(b)
+    where = lambda b, n: 3 * MIXED.index(b) + n % 3 if b in MIXED else (3 * PLAIN.index(b) + 2 if n == 1 else 6 + PLAIN.index(b))
+    group = {s: n for n, gs in enumerate(GROUPS) for s in gs}
+    turns = lambda n: PLAIN + MIXED
     t.wait_ge(S.df, 4)
-    for n in range(3):
-        for s in (2 * n, 2 * n + 1):
+    for n, gs in enumerate(GROUPS):
+        for s in gs:
             if s != r:
                 t.wait_ge(S["ar%d" % s], 2 * ne)
-        for b in (PLAIN + MIXED if n else MIXED[:1] + PLAIN + MIXED[1:]):
-            if b in PLAIN and n:
-                t.wait_ge(S["un%d" % b], n)
-            decode(bank(where(b, n), 2 * K), b, slice(2 * K * n, 2 * K * n + 2 * K), "mm%d" % n)
+        for b in turns(n):
+            if b in PLAIN and n > 1:
+                t.wait_ge(S["un%d" % b], n - 1)
+            elif n == 2:
+                t.wait_ge(S["uv%d" % PLAIN[MIXED.index(b)]], 1)
+            elif n == 3:
+                t.wait_ge(S["un%d" % b], 1)
+            decode(bank(where(b, n), K * len(gs)), b, slice(K * gs[0], K * gs[-1] + K), "mm%d" % n)
 
-    def unload(n, b, k, w):
-        a.wait_ge(S["mm%d" % n], k)
-        o = W * b + 8 + 2 * K * n
-        act(T.Y[:, o:o + w], bank(where(b, n), w), ev="un%d" % b)
+    def unload(n, b, q=a):
+        q.wait_ge(S["mm%d" % n], turns(n).index(b) + 1)
+        o, w = W * b + 8 + K * GROUPS[n][0], K * len(GROUPS[n])
+        if q is a:
+            act(T.Y[:, o:o + w], bank(where(b, n), w), ev="un%d" % b)
+        else:
+            cp(T.Y[:, o:o + w], bank(where(b, n), w), "uv%d" % b)
     tm = lambda b, s: T.TM[:, K * (2 * MIXED.index(b) + s % 2):K * (2 * MIXED.index(b) + s % 2) + K]
     pl = lambda s: T.PL[:, 16 * s:16 * s + L]
 
-    unload(0, MIXED[0], 1, K)
-    for k, b in enumerate(PLAIN):
-        v.wait_ge(S.mm0, 2 + k)
-        cp(T.Y[:, W * b + 8:W * b + 8 + 2 * K], bank(where(b, 0), 2 * K), "un%d" % b)
-    unload(0, MIXED[1], 4, K)
-    later = {1: [(1, PLAIN[0], 1), (1, PLAIN[1], 2)], 2: [(2, PLAIN[0], 1)], 3: [(2, PLAIN[1], 2)]}
+    for b in turns(0):
+        unload(0, b)
+    for b in PLAIN:
+        unload(1, b, v)
+    later = {1: [(2, PLAIN[0]), (2, PLAIN[1])], 2: [(3, PLAIN[0])], 3: [(3, PLAIN[1])]}
     a.wait_ge(S.u0, 4)
     v.wait_ge(S.u0, 4)
     for s in range(1, N):
@@ -451,20 +585,20 @@ def rank_program(g, core, T, topo):
         for b in MIXED:
             a.wait_ge(S["c%d" % b], s - 1) if s > 1 else a.wait_ge(S["un%d" % b], 1)
             act(tm(b, s), T.Y[:, W * b:W * b + 8 + K * s].indirect(pl(s)), ev="tm%d" % b)
-        for n, b, k in later.get(s, ()):
-            unload(n, b, k, 2 * K)
+        for n, b in later.get(s, ()):
+            unload(n, b)
         v.wait_ge(S["pl%d" % s], ne)
         for b in PLAIN + MIXED:
             o = W * b + 8 + K * s
+            n = group[s]
             if b in PLAIN:
-                v.wait_ge(S["un%d" % b], s // 2 + 1)
-                if s > 1:
-                    v.wait_ge(S["c%d" % b], s - 1)
+                v.wait_ge(S["un%d" % b], n)
+                v.wait_ge(S["c%d" % b], s - 1) if s > 1 else v.wait_ge(S["uv%d" % b], 1)
                 tt(T.Y[:, o:o + K], T.Y[:, W * b:o].indirect(pl(s)), T.Y[:, o:o + K], A.add, ev="c%d" % b)
             else:
-                v.wait_ge(S["mm%d" % (s // 2)], 4)
+                v.wait_ge(S["mm%d" % n], 4)
                 v.wait_ge(S["tm%d" % b], s)
-                z = 512 * where(b, s // 2) + K * (s % 2)
+                z = 512 * where(b, n) + K * GROUPS[n].index(s)
                 tt(T.Y[:, o:o + K], tm(b, s), T.PS[:, z:z + K], A.add, ev="c%d" % b)
 
     for q in (a, v):
@@ -483,19 +617,20 @@ def rank_program(g, core, T, topo):
 
     sy.wait_ge(S.nb, 1)
     sy.dma_start(T.ND[r], T.NB[0:1, :]).then_inc(S.nd, 16)
-    sy.dma_start(T.nb[r:r + 1, :], T.NB[0:1, 0:K]).then_inc(S.st, 16)
+    sy.wait_ge(S.nc, 1)
+    sy.dma_start(T.nb[:], T.NC[0:N, :]).then_inc(S.n0, 16)
     sy.wait_ge(S.so, 1)
     sy.dma_start(T.sc[:], T.SO[0:1, :]).then_inc(S.st, 16)
     sy.wait_ge(S.erx, 1)
-    sy.wait_ge(S.left, 2 * (n_on + ne))
+    sy.wait_ge(S.left, 2 * (n_on + ne) + ne * WIDE)
     sy.dma_start(T.er[:], T.ER[:]).then_inc(S.st, 16)
-    for s in range(N):
-        if s != r:
-            sy.wait_ge(S["li%d" % s], ne)
-            sy.dma_start(T.nb[s:s + 1, :], T.ND[s, 0:K // 2, :]).then_inc(S.st, 16)
+    g.wait_ge(S.li, ne * (N - 1))
+    g.wait_ge(S.n0, 16)
+    g.dma_start(T.nb[:], T.ND[:, 0:K // 2, :], accum_op=A.add).then_inc(S.n1, 16)
+    g.wait_ge(S.n1, 16)
     for h in range(4):
         sy.wait_ge(S["fv%d" % h], 2)
         sy.wait_ge(S["fa%d" % h], 2)
         sy.dma_start(T.acc[:, 512 * h:512 * h + 512], T.AC[:, 512 * h:512 * h + 512]).then_inc(S.st, 16)
     g.wait_ge(S.sent, sent[0])
-    sy.wait_ge(S.st, 16 * (N + 6))
+    sy.wait_ge(S.st, 16 * 6)

from concourse.bass import DstId, RemoteDMATransfer
from concourse.mybir import dt, AluOpType, ActivationFunctionType

N, TC, K = 6, 512, 160
W = 8 + N * K
L = K // 16
CORES_ALL = 128
HOST = [(1, 1, 1, (1, 2, 3)), (1, 0, 1, (0, 4, 5)), (2, 1, 2, (1, 4, 5)), (2, 0, 2, (0, 2, 3)), (3, 3, 1, range(N)), (4, 4, 1, range(N)), (5, 5, 1, (5, 0, 1)), (5, 4, 2, (4, 2, 3)), (0, 5, 2, range(N))]
HANDS = [3, 3, 3, 3, 3, 3]
EARLY = ()
LATE = (5, 0)
DELAY = 0
DELAY2 = 0
RING = True
SHARE = [(2, 1, 1, 1)] * N
ORDER = (0, 1, 2)
EARLY_E = 1
WIDE = True
SPLIT = False
GROUPS = [(0,), (1,), (2, 3), (4, 5)]
MIXED = (3, 2)
PLAIN = (0, 1)

F, B, I, U, C8, P8 = "float32", "bfloat16", "int32", "uint16", "float8_e4m3fn_x4", "uint8"
SCRATCH = {
    "U4": ("sbuf", [128, 16], B), "UT": ("sbuf", [128, 512], B),
    "UQ": ("sbuf", [128, 128], C8), "UP": ("sbuf", [128, 128], P8),
    "GR": ("sbuf", [128, 2048], B), "GQ": ("sbuf", [128, 512], C8), "GP": ("sbuf", [128, 512], P8),
    "ON": ("sbuf", [128, 516], B), "MM": ("sbuf", [128, 516], B),
    "EQ": ("sbuf", [128, 512], C8), "EP": ("sbuf", [128, 512], P8),
    "PS": ("psum", [128, 4096], F),
    "SR": ("sbuf", [128, 512], F), "SL": ("sbuf", [128, 512], F), "SCO": ("sbuf", [128, 4], F), "AS": ("sbuf", [128, 2], F),
    "HB": ("sbuf", [128, 2], F), "SG": ("sbuf", [128, 768], B), "CM": ("sbuf", [128, 1800], B), "CN": ("sbuf", [128, 1280], B),
    "OFF": ("sbuf", [128, 8], U), "DD": ("sbuf", [128, 64], F), "WW": ("sbuf", [128, 1072], F),
    "EB": ("sbuf", [128, 128], B), "EU": ("sbuf", [128, 128], B), "WB": ("sbuf", [128, 1072], B), "TH": ("sbuf", [128, 448], B),
    "TT": ("sbuf", [128, 448], F), "XX": ("sbuf", [128, 32], F), "ZZ": ("sbuf", [128, 80], F),
    "RM": ("sbuf", [128, 80], F), "SC": ("sbuf", [128, 80], F),
    "LT": ("sbuf", [128, 40], U), "LP": ("sbuf", [128, 16], U),
    "RO": ("sbuf", [128, 8], B), "RX": ("sbuf", [128, 8], B), "RK": ("sbuf", [128, 64], B), "RL": ("sbuf", [128, 4], U), "BA": ("sbuf", [128, 64], F),
    "Q0": ("sbuf", [128, 64], F), "Q1": ("sbuf", [128, 64], F), "OP": ("sbuf", [128, 4], F),
    "EX": ("sbuf", [128, 128], F), "ET": ("sbuf", [128, 128], F),
    "LQ": ("sbuf", [128, 64], F), "LA": ("sbuf", [128, 64], F), "LF": ("sbuf", [128, 32], F),
    "CG": ("sbuf", [128, 4 * K], B), "RC": ("sbuf", [128, N * K], C8), "RP": ("sbuf", [128, N * K], P8),
    "DF": ("sbuf", [128, 4 * K], F), "ER": ("sbuf", [128, 2048], F), "Y": ("sbuf", [128, 4 * W], F), "TM": ("sbuf", [128, 4 * K], F),
    "PL": ("sbuf", [128, 16 * N], U), "LL": ("sbuf", [128, 32], U), "AC": ("sbuf", [128, 2048], F), "IO": ("sbuf", [128, 512], F),
    "NB": ("sbuf", [128, 256], B), "ND": ("dram", [N, 128, 2], B), "NC": ("sbuf", [128, K], F), "SO": ("sbuf", [128, K], F),
    "VI": ("sbuf", [128, 32], I), "VJ": ("sbuf", [128, 32], I), "VK": ("sbuf", [128, 2], I), "UL": ("sbuf", [128, 32], U),
    "CF": ("sbuf", [128, 2], F), "SE": ("sbuf", [128, 2], U), "D0": ("sbuf", [128, 64], F),
    "DL": ("sbuf", [128, 1024], F),
    "TA": ("sbuf", [128, 32], F), "TB": ("sbuf", [128, 32], F),
}
_EV = ["v", "a", "mc", "ld_u", "on", "ul", "io1", "io2", "io3", "io4", "mst", "ut", "uq", "sco", "cnt", "sl", "er0", "xx", "za", "lt",
       "eq", "rks", "px", "lq", "ga", "lst", "qc", "df", "erx", "so", "nb", "nd", "ll", "st", "sent", "hp", "hc", "hl", "rk", "mo",
       "zy", "sr", "u0", "left", "mine", "rf", "dl", "li", "rkd", "nc", "n0", "n1"]
SEMAPHORES = _EV + ["%s%d" % (e, n) for e in ("ar", "pl") for n in range(N)] \
    + ["%s%d" % (e, n) for e in ("ld", "gq", "ms", "fv", "fa", "c", "tm", "mm", "un", "uv") for n in range(4)]

A, AF = AluOpType, ActivationFunctionType


def tracked(q, T, name):
    tot, pend = {}, {}

    def rec(ins, ev=None):
        e = ev or name
        ins.then_inc(T.sem[e], 1)
        tot[e] = tot.get(e, 0) + 1
        pend[e] = tot[e]

    def sync():
        for e in list(pend):
            q.wait_ge(T.sem[e], pend[e])
        pend.clear()
    return rec, sync


def calls(g, T):
    v, a = g.vector, g.scalar
    vr, vsync = tracked(v, T, "v")
    ar, async_ = tracked(a, T, "a")

    def ts(out, in0, s1, s2, op0, op1=None, ev=None):
        if op1 is None:
            vr(v.tensor_scalar(out, in0, s1, None, op0), ev)
        else:
            vr(v.tensor_scalar(out, in0, s1, s2, op0, op1), ev)

    def tt(out, x, y, op, ev=None):
        vr(v.tensor_tensor(out, x, y, op), ev)

    def cp(out, x, ev=None):
        vr(v.tensor_copy(out, x), ev)

    def act(out, x, func=AF.Copy, ev=None, **kw):
        ar(a.activation(out, x, func, **kw), ev)

    def iota(out, pattern, base, ev):
        g.iota(out, pattern, base, 0, allow_small_or_imprecise_dtypes=True).then_inc(T.sem[ev], 1)
    return vr, vsync, async_, ts, tt, cp, act, iota


def plan(T, topo, r):
    core = T.cores[r]
    others = [T.cores[(r - d) % N] for d in range(1, N)]
    hs = [c for c in topo.cores_of(core) if c != core and all(topo.may_write(c, d) for d in others)]
    hs.sort(key=lambda c: topo.die(c) == topo.die(core))
    if RING:
        ends = [sum(SHARE[r][:n]) for n in range(len(SHARE[r]) + 1)]
        cs = [core] + [hs[n] for n in ORDER]
        return others, [(c, others[x:y]) for c, x, y in zip(cs, ends, ends[1:])]
    direct, handed, _ = routes(T, topo)
    return others, [(core, direct[r])] + [(c, [d]) for c, d in zip(hs, handed[r])]


_ROUTES = []


def choices(options):
    if not options:
        return [[]]
    return [[x] + rest for rest in choices(options[1:]) for x in options[0]]


def routes(T, topo):
    if _ROUTES:
        return _ROUTES[0]
    cores = list(T.cores)
    chip = [topo.chip(c) for c in cores]
    side = {s: cores[d] for s in range(N) for d in range(N) if topo.mates(chip[s], chip[d])}
    taken = {s: [d for d in range(N) if d == s or topo.mates(chip[s], chip[d])] for s in range(N)}
    far, first = {}, {s: [] for s in range(N)}
    for d in range(N):
        if d not in side:
            idle = [c for c in range(CORES_ALL) if topo.mates(topo.chip(c), chip[d]) and topo.may_write(c, cores[d]) and topo.die(c) == topo.die(cores[d])][0]
            s = max(x for x in range(N) if topo.same_plane(chip[x], topo.chip(idle)))
            far[idle] = (s, cores[d])
            first[s].append(idle)
            taken[s].append(d)
    rest = [[d for d in range(N) if d not in taken[s]] for s in range(N)]
    pairs = [[(x, y) for x in rest[s] for y in rest[s] if x < y and topo.same_plane(chip[s], chip[x]) != topo.same_plane(chip[s], chip[y])]
             for s in range(N)]
    best = None
    for pick in choices(pairs):
        late = [[s for s in range(N) if d in pick[s]] for d in range(N)]
        if all(len(x) == 2 for x in late):
            soon = [[s for s in range(N) if d in rest[s] and d not in pick[s]] for d in range(N)]
            worth = sorted(max(x) for x in soon + late)
            if best is None or worth > best[0]:
                best = (worth, pick, soon, late)
    _, pick, soon, late = best
    direct = [[cores[d] for d in range(N) if min(soon[d]) == s] + first[s] + ([side[s]] if s in side else [])
              + [cores[d] for d in range(N) if max(soon[d]) == s] for s in range(N)]
    handed = [[cores[d] for d in sorted(pick[s], key=lambda d: max(late[d]) == s)] for s in range(N)]
    _ROUTES.append((direct, handed, far))
    return _ROUTES[0]


def listers(T, topo):
    return {plan(T, topo, r)[1][n][0]: (s, to) for s, r, n, to in HOST}


def list_of(T, topo, c):
    return listers(T, topo).get(c, (None,))[0]


def rank_roads(T, topo, r):
    hs = [c for c, _ in plan(T, topo, r)[1][1:]]
    users = {c: s for c, (s, _) in listers(T, topo).items() if s == 0 or s >= r}
    late = [c for c, s in users.items() if c not in hs and s in LATE]
    jobs = {c: late[n::HANDS[r]] if n < HANDS[r] else [] for n, c in enumerate(hs)}
    return [c for c, s in users.items() if c not in hs and s not in LATE], {c: x for c, x in jobs.items() if x or c in users}


def slot(T, r, s):
    return T.RO[:, 0:4] if s == r > 0 else T.RK[:, 8 * r + 8:8 * r + 12]


def landing(T, topo, r, c):
    s = list_of(T, topo, c)
    return slot(T, r, s) if s is not None and (s == 0 or s >= r) else T.RX[:, 0:4]


def transfer(topo, src, cores, mask, sem, dsts=None):
    ids = [DstId(rid=topo.addr(d)[0], pnc=topo.addr(d)[1]) for d in cores]
    return RemoteDMATransfer(dst_ids=ids, dma_engine_mask=mask, remote_sem=sem, srcs=[src], dsts=dsts or [src] * len(cores))


def table(g, T, C, even, odd, step):
    vr, vsync, async_, ts, tt, cp, act, iota = C
    iota(T.TA[:, 0:16], even[0], even[1], "io2")
    iota(T.TA[:, 16:32], odd[0], odd[1], "io2")

    def finish():
        g.vector.wait_ge(T.sem.io2, 2)
        vr(g.vector.transpose(T.TB[:], T.TA[:]))
        vsync()
        ts(T.SE[:, 0:1], T.TB[:, 0:1], 0.0, None, A.add)
        ts(T.SE[:, 1:2], T.TB[:, 0:1], float(step), None, A.add)
    return finish


def permute_tables(g, T, C, col, ww, turned):
    vr = C[0]
    fin = table(g, T, C, ([[32, 4], [192, 2], [16, 2]], col), ([[32, 4], [-160, 2], [16, 2]], 160 + col), 128)
    v = g.vector
    vr(v.memset(ww[:, 0:192], 0.0))
    vr(v.memset(turned[:, 352:448], 0.0))
    vr(v.memset(T.RM[:], 1.0))
    C[1]()
    vr(v.memset(T.RM[:, 0:80:8], 0.0))
    return fin


def permute(g, T, C, val, n, ww, turned):
    vr, vsync, async_, ts, tt, cp, act, iota = C
    v, a = g.vector, g.scalar
    cp(ww[:].indirect(T.OFF[:, 0:n]), val)
    vsync()
    vr(v.transpose(turned[:, 0:160], ww[:, 16:176]))
    vr(v.transpose(turned[:, 160:352], ww[:, 0:192]))
    vsync()
    cp(T.XX[:], turned[:].indirect(T.SE[:]), "xx")
    vsync()
    a.wait_ge(T.sem.xx, 1)
    cp(T.ZZ[:, 0:80:4], T.XX[:, 0:20])
    for p in (0, 64):
        cp(T.ZZ[64 - p:128 - p, 2:80:4], T.XX[p:p + 64, 0:20])
    for d in (1, 3):
        for p in range(4):
            o = 32 * (p ^ d)
            dst, src = T.ZZ[o:o + 32, d:80:4], T.XX[32 * p:32 * p + 32, 0:20]
            if d == 1 and p < 3:
                cp(dst, src)
            else:
                act(dst, src, ev="za")
    vsync()
    v.wait_ge(T.sem.za, 5)
    vr(v.tensor_tensor_scan(T.SC[:], T.RM[:], T.ZZ[:], 0.0, A.mult, A.add))
    vsync()
    return T.SC[:, 7:80:8]


def make_list(g, T, s, ne, near):
    C = calls(g, T)
    vr, vsync, async_, ts, tt, cp, act, iota = C
    v, a, S = g.vector, g.scalar, T.sem
    m = s or N
    g.iota(T.VI[:, 0:4], [[1, 4]], 0, 8).then_inc(S.io1, 1)
    short = 0 < s and 8 + K * s <= TC
    mid = 8 + K * s if short else 0
    ex, et, ww, turned = (T.EB, T.EU, T.WB, T.TH) if short else (T.EX, T.ET, T.WW, T.TT)
    iota(T.BA[:], [[0, 8], [2 * K, 8]], 2 * 8 + TC - 2 * K - mid, "io3")
    vr(v.memset(T.HB[:, 0:1], 4096.0 * (2 * K - TC - 1)), "ul")
    if s:
        fin = permute_tables(g, T, C, 14, ww, turned)
    else:
        fin = table(g, T, C, ([[1, 8], [32, 2]], 0), ([[1, 8], [-32, 2]], 32), 8)
        vr(v.memset(T.LQ[:, 16:32], 0.0))
    vr(v.memset(T.RK[:, 0:8], float(2 * K - 2 * 8 - TC)))
    vr(v.memset(T.RK[:, 8 * m + 8:64], 0.0))
    vr(v.memset(ex[:], 0.0))
    v.wait_ge(S.io1, 1)
    ts(T.VJ[:, 0:4], T.VI[:, 0:4], 63, None, A.bitwise_and)
    ts(T.VK[:, 0:1], T.VI[:, 0:1], 128, None, A.bitwise_and)
    vsync()
    cp(T.RL[:], T.VJ[:, 0:4], "ul")
    cp(T.CF[:, 0:1], T.VK[:, 0:1])
    fin()
    ts(T.OP[:, 0:1], T.CF[:, 0:1], 528 / 128, 272.0, A.mult, A.add)
    ts(T.OP[:, 1:2], T.CF[:, 0:1], -528 / 128, 800.0, A.mult, A.add)
    vsync()
    v.wait_ge(S.io3, 1)
    arrive = ne * ((m + 1 if s else m) - bool(near))
    v.wait_ge(S.rk, arrive)
    if near:
        v.wait_ge(S.rf, near)
    if DELAY and s in LATE:
        vr(v.memset(T.ER[:, 0:DELAY], 0.0))
    win = T.RK[:].indirect(T.RL[:])
    a.wait_ge(S.ul, 2)
    a.wait_ge(S.rk, arrive)
    if near:
        a.wait_ge(S.rf, near)
    act(T.Q0[:], win, AF.Relu, "mo", bias=T.HB[:, 0:1], scale=-4096.0)
    tt(T.Q1[:], win, T.BA[:], A.add)
    for h in range(2 if s else 0):
        ts(T.OFF[:, h:8:2], T.RO[:, 0:4], 0.5, T.OP[:, h:h + 1], A.mult, A.add)
    vsync()
    v.wait_ge(S.mo, 1)
    vr(v.tensor_tensor_scan(ex[:, 0:128:2], T.Q0[:], T.Q1[:], 0.0, A.add, A.min), "px")
    if s:
        vsync()
        vr(v.transpose(et[:], ex[:]))
        vsync()
        out = T.PL[:, 16 * s:16 * s + L]
        ts(out, permute(g, T, C, et[:], 8, ww, turned), 0.5, mid / 2, A.mult, A.add, ev="hl")
        vsync()
        return out, "pl%d" % s
    vsync()
    a.wait_ge(S.px, 1)
    for p in range(4):
        for d in range(4):
            dst, src = T.LQ[32 * d:32 * d + 32, p:16:4], T.EX[32 * p:32 * p + 32, 14:128:32]
            if d < 2:
                cp(dst, src)
            else:
                act(dst, src, ev="lq")
    vsync()
    v.wait_ge(S.lq, 8)
    for h in range(2):
        vr(v.transpose(T.LA[:, 32 * h:32 * h + 32], T.LQ[:, 0:32]))
    vsync()
    vr(v.transpose(T.LQ[:, 32:64], T.LA[:, 16:48]))
    vsync()
    ts(T.LF[:], T.LQ[:].indirect(T.SE[:]), 0.5, None, A.mult)
    vsync()
    cp(T.LL[:], T.LF[:], "hl")
    vsync()
    return T.LL[:], "ll"


def helper_program(g, core, T, topo):
    S = T.sem
    if not RING and core in routes(T, topo)[2]:
        r, to = routes(T, topo)[2][core]
        ne = len(topo.engines(core, to))
        g.wait_ge(S["ar%d" % r], 2 * len(topo.engines(T.cores[r], core)))
        for src in (T.RP[:, K * r:K * r + K], T.RC[:, K * r:K * r + K].bitcast(dt.uint8)):
            g.remote_dma_fused([transfer(topo, src, [to], topo.mask(core, to), S["ar%d" % r])], local_sem=S.sent)
        g.wait_ge(S.sent, 2 * ne)
    for r in range(N):
        if topo.chip(T.cores[r]) != topo.chip(core):
            continue
        others, roads = plan(T, topo, r)
        mask, ne = topo.mask(core, others[0]), len(topo.engines(core, others[0]))
        nin = len(topo.engines(T.cores[r], core)) - ne
        own = slice(K * r, K * r + K)
        dests = dict(roads[1:]).get(core)
        if dests is None:
            continue
        jobs = [("hc", nin + ne * WIDE, T.RC[:, own].bitcast(dt.uint8), dests, "ar%d" % r, None), ("hp", nin, T.RP[:, own], dests, "ar%d" % r, None)] if dests else []
        s = list_of(T, topo, core)
        here = LATE and s is not None and (s == 0 or s >= r)
        if s is not None:
            src, sem = make_list(g, T, s, ne, nin if here else 0)
            jobs.insert(0 if s in EARLY else 2, ("hl", 1, src, [T.cores[d] for d in listers(T, topo)[core][1]], sem, None))
        if core in rank_roads(T, topo, r)[1]:
            late = rank_roads(T, topo, r)[1][core]
            jobs.insert(0, ("rf", nin, landing(T, topo, r, core), late, "rk", [slot(T, r, list_of(T, topo, x)) for x in late]))
        for wait, n, src, to, sem, dsts in jobs:
            g.wait_ge(S[wait], n)
            if SPLIT and wait == "hc":
                g.remote_dma_fused([transfer(topo, T.RC[:, K * r + 80 * h:K * r + 80 * h + 80].bitcast(dt.uint8), to, mask & m, S[sem]) for h, m in enumerate((0x0F0F, 0xF0F0))], local_sem=S.sent)
            elif wait == "hl":
                g.remote_dma_fused([transfer(topo, src, [c for c in to if c in others], mask, S[sem]),
                                    transfer(topo, src, [T.cores[r]], topo.mask(core, T.cores[r]) & ~mask, S[sem])], local_sem=S.sent)
            elif to:
                g.remote_dma_fused([transfer(topo, src, to, mask, S[sem], dsts)], local_sem=S.sent)
        g.wait_ge(S.sent, sum(ne + nin * (job[0] == "hl") for job in jobs if job[3]))


def rank_program(g, core, T, topo):
    r = T.rank_of(core)
    if r is None:
        return helper_program(g, core, T, topo)
    v, a, t, sy = g.vector, g.scalar, g.tensor, g.sync
    S = T.sem
    C = calls(g, T)
    vr, vsync, async_, ts, tt, cp, act, iota = C
    blk = lambda b: slice(128 * b, 128 * b + 128)
    bank = lambda n, w: T.PS[:, 512 * n:512 * n + w]

    a.dma_start(T.U4[:, 0:4], T.u[:, 0:4]).then_inc(S.ld_u, 16)
    for q in range(4):
        (a if q % 2 else sy).dma_start(T.GR[:, 512 * q:512 * q + 512], T.gr[:, 512 * q:512 * q + 512]).then_inc(S["ld%d" % q], 16)

    g.iota(T.VI[:], [[0, 32]], 0, 1).then_inc(S.io1, 1)
    vr(v.memset(T.ON[:], 1.0), "on")
    fin = permute_tables(g, T, C, 0, T.WB, T.TH)
    iota(T.D0[:], [[128, 4], [1, 16]], -256, "io3")
    g.wait_ge(S.on, 1)
    g.affine_select(T.MM[:], T.ON[:], [[-1, 516]], A.is_equal, 0.0, 3, 4).then_inc(S.mst, 1)
    g.dma_start(T.ER[:], T.gr[:]).then_inc(S.er0, 16)
    v.wait_ge(S.io1, 1)
    ts(T.VJ[:], T.VI[:], 3, None, A.bitwise_and)
    ts(T.VK[:], T.VI[:, 0:2], 112, None, A.bitwise_and)
    at = {0: 0, 3: 260, 1: 520, 2: 1160}
    for b in (0, 3):
        vr(v.memset(T.CM[:, at[b] + 256:at[b] + 260], -32.0))
    vr(v.memset(T.HB[:, 0:1], -0.5))
    vr(v.memset(T.HB[:, 1:2], 0.5), "zy")
    vsync()
    cp(T.UL[:], T.VJ[:], "ul")
    cp(T.CF[:], T.VK[:])
    fin()
    v.wait_ge(S.io3, 1)
    ts(T.DD[:], T.D0[:], T.CF[:, 0:1], None, A.add)
    a.wait_ge(S.on, 1)
    for b in range(4):
        act(T.Y[:, W * b:W * b + 8], T.ON[:, 0:8], ev="u0", scale=0.0)

    def ones(b):
        v.wait_ge(S.mst, 1)
        vr(v.quantize_mx(T.EQ[:, blk(b)], T.EP[:, blk(b)], T.MM[:, 3 - b:515 - b]), "eq")

    for q in (a, v):
        q.wait_ge(S.ld_u, 16)
    a.wait_ge(S.ul, 1)
    act(T.UT[:, 256:512], T.U4[:, 0:4].indirect(T.UL[:, 16:32]), ev="ut")
    cp(T.UT[:, 0:256], T.U4[:, 0:4].indirect(T.UL[:, 0:16]), "ut")
    for q in range(4):
        v.wait_ge(S["ld%d" % q], 16)
        vr(v.quantize_mx(T.GQ[:, blk(q)], T.GP[:, blk(q)], T.GR[:, 512 * q:512 * q + 512]), "gq%d" % q)
        if q == 0:
            v.wait_ge(S.ut, 2)
            vr(v.quantize_mx(T.UQ[:], T.UP[:], T.UT[:]), "uq")
        elif q - 1 < EARLY_E:
            ones(q - 1)
    t.wait_ge(S.uq, 1)
    for q in range(4):
        t.wait_ge(S["gq%d" % q], 1)
        t.matmul_mx(bank(q, 128), T.UQ[:], T.UP[:], T.GQ[:, blk(q)], T.GP[:, blk(q)], True, True).then_inc(S["ms%d" % q], 1)
        t.matmul_mx(bank(4 + q, 128), T.GQ[:, blk(q)], T.GP[:, blk(q)], T.UQ[:], T.UP[:], True, True).then_inc(S.mc, 1)
    for q in range(4):
        a.wait_ge(S["ms%d" % q], 1)
        act(T.SR[:, blk(q)], bank(q, 128), AF.Abs, "sr")
        if q % 2:
            a.wait_ge(S.mc, q + 1)
            act(T.SCO[:, q - 1:q + 1], T.PS[:, 512 * (3 + q):512 * (5 + q):512], AF.Abs, "sco")
    for h in range(2):
        g.wait_ge(S.sr, 2 * h + 2)
        g.affine_select(T.SL[:, 256 * h:256 * h + 256], T.SR[:, 256 * h:256 * h + 256], [[0, 2], [-1, 128]], A.is_gt, -1.0, 0, 1).then_inc(S.sl, 1)

    iota(T.NC[0:32, :], [[0, K]], 256, "nc")

    async_()
    for h, (b, lo) in enumerate(((0, 128), (3, 0))):
        act(T.SG[:, 384 * h:384 * h + 384], T.SR[:, lo:lo + 384], AF.Sign, "a" if h else "mo", bias=T.SCO[:, b:b + 1], scale=-1.0)
    a.wait_ge(S.zy, 1)
    for h in range(2):
        a.wait_ge(S.mo, 1) if h == 0 else async_()
        sg = T.SG[:, 384 * h:384 * h + 384]
        act(sg, sg, AF.Sign, "cnt", bias=T.HB[:, h:h + 1], scale=-1.0, accum_out=T.AS[:, h:h + 1])

    def cmp(b, z, src, op):
        ts(T.CM[:, at[b] + z:at[b] + z + src.stop - src.start], (T.SL if op == A.is_equal else T.SR)[:, src], T.SCO[:, b:b + 1], 2.0, op, A.mult)

    def count(b, n, first):
        z = at[b]
        vr(v.tensor_tensor_scan(T.CN[:, 320 * b + 320 - n:320 * b + 320], T.CM[:, z:z + n], T.CM[:, z + n:z + 2 * n], first, A.add, A.add), "rkd")
    v.wait_ge(S.sr, 2)
    v.wait_ge(S.sco, 1)
    cmp(0, 0, blk(0), A.is_gt)
    cmp(1, 0, blk(0), A.is_ge)
    cmp(1, 128, blk(1), A.is_gt)
    v.wait_ge(S.sr, 4)
    cmp(1, 256, slice(256, 512), A.is_gt)
    v.wait_ge(S.sco, 2)
    cmp(2, 0, slice(0, 256), A.is_ge)
    v.wait_ge(S.sl, 1)
    cmp(1, 512, blk(1), A.is_equal)
    cmp(0, 128, blk(0), A.is_equal)
    cmp(2, 256, slice(256, 512), A.is_gt)
    cmp(3, 0, blk(3), A.is_gt)
    v.wait_ge(S.sl, 2)
    cmp(2, 512, blk(2), A.is_equal)
    vsync()
    cmp(3, 128, blk(3), A.is_equal)
    count(1, 320, -512.0)
    count(2, 320, -512.0)
    vsync()
    for h, b in enumerate((0, 3)):
        v.wait_ge(S.cnt, h + 1)
        count(b, 130, T.AS[:, h:h + 1])
    vsync()
    rk = T.CN[:, 319:1280:320]
    ts(T.OFF[:, 0:4], rk, 0.5, 272.0, A.mult, A.add)
    vsync()
    a.wait_ge(S.rkd, 4)
    act(T.RO[:, 0:4], rk, ev="rks")
    num = permute(g, T, C, T.DD[:], 4, T.WB, T.TH)
    for k in (2, 3, 0, 1):
        ts(T.LT[:, L * k:L * k + L], num, 4.0, float(1024 + k), A.mult, A.add, ev="lt")

    for k in (2, 3):
        a.wait_ge(S.lt, k - 1)
        act(T.CG[:, k:4 * K:4], T.GR[:].indirect(T.LT[:, L * k:L * k + L]), ev="ga")
    for k in (0, 1):
        v.wait_ge(S.lt, k + 3)
        cp(T.CG[:, k:4 * K:4], T.GR[:].indirect(T.LT[:, L * k:L * k + L]))
    vsync()
    v.wait_ge(S.ga, 2)
    own = slice(K * r, K * r + K)
    vr(v.quantize_mx(T.RC[:, own], T.RP[:, own], T.CG[:]), "qc")
    for b in range(EARLY_E, 4):
        ones(b)
    ts(T.LP[:, 0:L], num, 256.0, None, A.add, ev="lst")
    ts(T.LP[:, L:16], T.SC[:, 7:55:8], 256.0, None, A.add, ev="lst")

    others, roads = plan(T, topo, r)
    off, ne = topo.mask(core, others[0]), len(topo.engines(core, others[0]))
    hs = [c for c, d in roads[1:] if d]
    on, n_on = topo.mask(core, roads[1][0]) & ~off, len(topo.engines(core, roads[1][0])) - ne
    sent = [0]

    def send(trs, n):
        g.remote_dma_fused(trs, local_sem=S.sent)
        sent[0] += n
    early, late = rank_roads(T, topo, r)
    trs = [transfer(topo, T.RO[:, 0:4], list(late), on, S.rf, [landing(T, topo, r, c) for c in late])] if late else []
    if early:
        trs.append(transfer(topo, T.RO[:, 0:4], early, off, S.rk, [slot(T, r, list_of(T, topo, c)) for c in early]))
    g.wait_ge(S.rks, 1)
    send(trs, n_on * bool(late) + ne * bool(early))
    g.wait_ge(S.qc, 1)
    if DELAY2:
        iota(T.DL[:, 0:DELAY2], [[1, DELAY2]], 0, "dl")
        g.wait_ge(S.dl, 1)
    planes, codes, direct = T.RP[:, own], T.RC[:, own].bitcast(dt.uint8), (roads[0][1], off, S["ar%d" % r])
    for call in ([(codes, hs, on | off * WIDE, S.hc)], [(planes, hs, on, S.hp), (planes,) + direct], [(codes,) + direct]):
        if any(w[1] for w in call):
            if SPLIT and call[0][0] is codes:
                call = [(T.RC[:, K * r + 80 * h:K * r + 80 * h + 80].bitcast(dt.uint8), call[0][1], call[0][2] & m, call[0][3]) for h, m in enumerate((0x0F0F, 0xF0F0))]
            g.remote_dma_fused([transfer(topo, *w) for w in call if w[1]], local_sem=S.left)
    iota(T.IO[:], [[1, 512]], -256, "io4")
    g.wait_ge(S.nd, 16)
    send([transfer(topo, T.ND[r], others, off, S.li)], ne)

    def decode(out, b, cols, ev):
        t.matmul_mx(out, T.EQ[:, blk(b)], T.EP[:, blk(b)], T.RC[:, cols], T.RP[:, cols], True, True).then_inc(S[ev], 1)
    t.wait_ge(S.qc, 1)
    t.wait_ge(S.sr, 4)
    t.wait_ge(S.sco, 2)
    for b in range(4):
        t.wait_ge(S.eq, b + 1)
        decode(bank(b, K), b, own, "mine")
    for b in range(4):
        v.wait_ge(S.mine, b + 1)
        tt(T.DF[:, K * b:K * b + K], T.CG[:, b:4 * K:4], bank(b, K), A.subtract, ev="df")
    vsync()
    v.wait_ge(S.er0, 16)
    cp(T.ER[:].indirect(T.LT[:, 0:40]), T.DF[:], "erx")

    a.wait_ge(S.io4, 1)
    a.wait_ge(S.lst, 2)
    act(T.NB[:], T.IO[:].indirect(T.LP[:]), ev="nb")
    act(T.SO[:], T.SR[:].indirect(T.LP[:, 0:L]), ev="so")

    where = lambda b, n: 3 * MIXED.index(b) + n % 3 if b in MIXED else (3 * PLAIN.index(b) + 2 if n == 1 else 6 + PLAIN.index(b))
    group = {s: n for n, gs in enumerate(GROUPS) for s in gs}
    turns = lambda n: PLAIN + MIXED
    t.wait_ge(S.df, 4)
    for n, gs in enumerate(GROUPS):
        for s in gs:
            if s != r:
                t.wait_ge(S["ar%d" % s], 2 * ne)
        for b in turns(n):
            if b in PLAIN and n > 1:
                t.wait_ge(S["un%d" % b], n - 1)
            elif n == 2:
                t.wait_ge(S["uv%d" % PLAIN[MIXED.index(b)]], 1)
            elif n == 3:
                t.wait_ge(S["un%d" % b], 1)
            decode(bank(where(b, n), K * len(gs)), b, slice(K * gs[0], K * gs[-1] + K), "mm%d" % n)

    def unload(n, b, q=a):
        q.wait_ge(S["mm%d" % n], turns(n).index(b) + 1)
        o, w = W * b + 8 + K * GROUPS[n][0], K * len(GROUPS[n])
        if q is a:
            act(T.Y[:, o:o + w], bank(where(b, n), w), ev="un%d" % b)
        else:
            cp(T.Y[:, o:o + w], bank(where(b, n), w), "uv%d" % b)
    tm = lambda b, s: T.TM[:, K * (2 * MIXED.index(b) + s % 2):K * (2 * MIXED.index(b) + s % 2) + K]
    pl = lambda s: T.PL[:, 16 * s:16 * s + L]

    for b in turns(0):
        unload(0, b)
    for b in PLAIN:
        unload(1, b, v)
    later = {1: [(2, PLAIN[0]), (2, PLAIN[1])], 2: [(3, PLAIN[0])], 3: [(3, PLAIN[1])]}
    a.wait_ge(S.u0, 4)
    v.wait_ge(S.u0, 4)
    for s in range(1, N):
        a.wait_ge(S["pl%d" % s], ne)
        for b in MIXED:
            a.wait_ge(S["c%d" % b], s - 1) if s > 1 else a.wait_ge(S["un%d" % b], 1)
            act(tm(b, s), T.Y[:, W * b:W * b + 8 + K * s].indirect(pl(s)), ev="tm%d" % b)
        for n, b in later.get(s, ()):
            unload(n, b)
        v.wait_ge(S["pl%d" % s], ne)
        for b in PLAIN + MIXED:
            o = W * b + 8 + K * s
            n = group[s]
            if b in PLAIN:
                v.wait_ge(S["un%d" % b], n)
                v.wait_ge(S["c%d" % b], s - 1) if s > 1 else v.wait_ge(S["uv%d" % b], 1)
                tt(T.Y[:, o:o + K], T.Y[:, W * b:o].indirect(pl(s)), T.Y[:, o:o + K], A.add, ev="c%d" % b)
            else:
                v.wait_ge(S["mm%d" % n], 4)
                v.wait_ge(S["tm%d" % b], s)
                z = 512 * where(b, n) + K * GROUPS[n].index(s)
                tt(T.Y[:, o:o + K], tm(b, s), T.PS[:, z:z + K], A.add, ev="c%d" % b)

    for q in (a, v):
        q.wait_ge(S.ll, ne)
    for h in range(4):
        for b in range(4):
            dst, win = T.AC[:, 512 * h + b:512 * h + 512:4], T.Y[:, W * b:W * b + W].indirect(T.LL[:, 8 * h:8 * h + 8])
            if h == 0:
                (a if b in PLAIN else v).wait_ge(S["c%d" % b], N - 1)
            if b in PLAIN:
                act(dst, win, ev="fa%d" % h)
            else:
                cp(dst, win, "fv%d" % h)
    vsync()
    async_()

    sy.wait_ge(S.nb, 1)
    sy.dma_start(T.ND[r], T.NB[0:1, :]).then_inc(S.nd, 16)
    sy.wait_ge(S.nc, 1)
    sy.dma_start(T.nb[:], T.NC[0:N, :]).then_inc(S.n0, 16)
    sy.wait_ge(S.so, 1)
    sy.dma_start(T.sc[:], T.SO[0:1, :]).then_inc(S.st, 16)
    sy.wait_ge(S.erx, 1)
    sy.wait_ge(S.left, 2 * (n_on + ne) + ne * WIDE)
    sy.dma_start(T.er[:], T.ER[:]).then_inc(S.st, 16)
    g.wait_ge(S.li, ne * (N - 1))
    g.wait_ge(S.n0, 16)
    g.dma_start(T.nb[:], T.ND[:, 0:K // 2, :], accum_op=A.add).then_inc(S.n1, 16)
    g.wait_ge(S.n1, 16)
    for h in range(4):
        sy.wait_ge(S["fv%d" % h], 2)
        sy.wait_ge(S["fa%d" % h], 2)
        sy.dma_start(T.acc[:, 512 * h:512 * h + 512], T.AC[:, 512 * h:512 * h + 512]).then_inc(S.st, 16)
    g.wait_ge(S.sent, sent[0])
    sy.wait_ge(S.st, 16 * 6)
